import numpy as np
import ml_dtypes


def mxq(x, axis, fmt="e4m3"):
    dtype, down = {"e4m3": (ml_dtypes.float8_e4m3fn, 7), "e5m2": (ml_dtypes.float8_e5m2, 14)}[fmt]
    v = np.moveaxis(np.asarray(x, np.float32).astype(ml_dtypes.bfloat16).astype(np.float64), axis, -1)
    blocks = v.reshape(v.shape[:-1] + (-1, 32))
    amax = np.abs(blocks).max(-1, keepdims=True)
    byte = np.maximum(np.where(amax > 0, np.frexp(amax)[1] - 1 + 127, 0) - down, 1)
    scale = np.exp2(byte - 127.0)
    codes = (blocks / scale).astype(np.float32).astype(dtype).astype(np.float64)
    return np.moveaxis((codes * scale).reshape(v.shape), -1, axis)


WIDE = False


def mx_kscale(k):
    if not WIDE:
        return np.ones(k)
    levels = np.array([10, -10, 5, -5, 0])
    if k % 512:
        return np.exp2(np.random.permutation(np.resize(levels, k // 32))).repeat(32)
    a = np.empty((k // 512, 16))
    for p in range(k // 512):
        a[p, :8] = np.random.permutation(np.resize(levels, 8))
        for g in range(8):
            far = levels[np.abs(levels - a[p, g]) >= 10]
            a[p, g + 8] = far[np.random.randint(len(far))]
    return np.exp2(a.ravel()).repeat(32)


BF16 = ml_dtypes.bfloat16


def bf(x):
    return np.asarray(x, np.float32).astype(BF16)


def f64(x):
    return np.asarray(x).astype(np.float64)

def planes(Y):
    n, m = Y.shape
    b = f64(bf(Y)).reshape(n // 32, 32, m)
    amax = np.abs(b).max(1)
    byte = np.clip(np.where(amax > 0, np.frexp(amax)[1] - 1 + 127 - 7, 1), 1, 254)
    codes = (b * np.exp2(127.0 - byte)[:, None, :]).reshape(n, m).astype(np.float32).astype(ml_dtypes.float8_e4m3fn).view(np.uint8)
    words = codes.reshape(n // 512, 128, 4, m).transpose(0, 1, 3, 2)
    return np.ascontiguousarray(words), np.ascontiguousarray(byte.astype(np.uint8).reshape(n // 512, 16, m))


M, DS, DT, V = 1024, 1024, 2048, 1536


def setup_inputs():
    s = mx_kscale(DS)
    t = mx_kscale(DT)
    h_student = np.random.randn(M, DS) * s[None, :]
    w_student = np.random.randn(DS, V) * (1.5 / np.sqrt(DS)) / s[:, None]
    h_teacher = np.random.randn(M, DT) * t[None, :]
    w_teacher = np.random.randn(DT, V) * (1.5 / np.sqrt(DT)) / t[:, None]
    class_w = 2.0 * np.exp(0.8 * np.random.randn(V))
    return {
        "h_student": bf(h_student),
        "w_student": bf(w_student),
        "h_teacher": bf(h_teacher),
        "w_teacher": bf(w_teacher),
        "class_w": bf(class_w),
    }

def reference(h_student, w_student, h_teacher, w_teacher, class_w):
    zs = mxq(f64(h_student), 1, "e4m3") @ mxq(f64(w_student), 0, "e4m3")
    zt = mxq(f64(h_teacher), 1, "e4m3") @ mxq(f64(w_teacher), 0, "e4m3")
    ps = 1.0 / (1.0 + np.exp(-zs))
    pt = 1.0 / (1.0 + np.exp(-zt))
    y = (ps - pt) * f64(class_w)[None, :]
    Y = y.reshape(M, V).T
    words, scales = planes(Y)
    return y, words, scales

@@ -1,0 +1,375 @@
+from contextlib import ExitStack
+
+import concourse.mybir as mybir
+from concourse.masks import make_identity
+
+M, DS, DT, V = 1024, 1024, 2048, 1536
+FLOPS = 2 * M * V * (DS + DT)
+
+F32 = mybir.dt.float32
+BF16 = mybir.dt.bfloat16
+I32 = mybir.dt.int32
+U32 = mybir.dt.uint32
+U8 = mybir.dt.uint8
+FP8X4 = mybir.dt.float8_e4m3fn_x4
+SIGMOID = mybir.ActivationFunctionType.Sigmoid
+
+P = 128
+PACK = 4
+K_PASS = P * PACK
+S_PASSES = DS // K_PASS
+PASSES = (DS + DT) // K_PASS
+M_TILES = M // P
+CHUNK = 256
+CHUNKS = V // CHUNK
+GROUP = 512
+GROUPS = V // GROUP
+BANK = 512
+H_BANKS = PASSES // 2
+
+
+def tile_distill_logit_grad_g1_kernel(tc, h_student, w_student, h_teacher, w_teacher, class_w, out_0, out_1, out_2):
+    nc = tc.nc
+    with ExitStack() as ctx:
+        sb = ctx.enter_context(tc.tile_pool(name="sb", bufs=1))
+        ps = ctx.enter_context(tc.psum_pool(name="ps", bufs=1))
+        ctx.enter_context(tc.manual_schedule())
+
+        def ring(name, depth, index, shape, dtype):
+            return sb.tile(shape, dtype, name=name, tag="%s%d" % (name, index % depth), align_bytes=64)
+
+        def bank(index):
+            return ps.tile([P, BANK], F32, name="bank", tag="bank%d" % index)
+
+        def copy_on(engine, out, in_):
+            if engine == "scalar":
+                nc.scalar.copy(out=out, in_=in_)
+            else:
+                nc.vector.tensor_copy(out=out, in_=in_)
+
+        ident = sb.tile([P, P], F32, name="ident")
+        make_identity(nc, ident[:])
+        warm_in = sb.tile([P, 1], F32, name="warm_in")
+        warm_out = sb.tile([P, 1], F32, name="warm_out")
+        nc.vector.memset(warm_in[:], 0.0)
+        nc.scalar.activation(out=warm_out[:], in_=warm_in[:], func=SIGMOID)
+
+        h_raw, h_banks, h_grouped, h_codes, h_scales = {}, {}, {}, {}, {}
+        w_raw, w_grouped, w_codes, w_scales, cw = {}, {}, {}, {}, {}
+        logits, probs, diffs, ys, y_pairs, y_banks, y_grouped, y_codes, y_scales = {}, {}, {}, {}, {}, {}, {}, {}, {}
+
+        def load_hs(m):
+            t = ring("hs", 4, m, [P, DS], BF16)
+            nc.sync.dma_start(out=t[:], in_=h_student[m * P:(m + 1) * P, :])
+            h_raw[m, 0] = t[:].bitcast(F32)
+
+        def load_ht(m):
+            t = ring("ht", 4, m, [P, DT], BF16)
+            nc.sync.dma_start(out=t[:], in_=h_teacher[m * P:(m + 1) * P, :])
+            words = t[:].bitcast(F32)
+            h_raw[m, 1] = words[:, 0:BANK]
+            h_raw[m, 2] = words[:, BANK:2 * BANK]
+
+        def load_h(m):
+            load_hs(m)
+            load_ht(m)
+
+        def load_w(k, first_chunk, chunks, slot):
+            rows = w_student[k * K_PASS:(k + 1) * K_PASS, :] if k < S_PASSES else w_teacher[(k - S_PASSES) * K_PASS:(k - S_PASSES + 1) * K_PASS, :]
+            cols = slice(first_chunk * CHUNK, (first_chunk + chunks) * CHUNK)
+            t = ring("wraw", 2 * PASSES, slot, [P, PACK, chunks * CHUNK], BF16)
+            nc.sync.dma_start(out=t[:], in_=rows[:, cols].rearrange("(p j) c -> p j c", j=PACK))
+            for i in range(chunks):
+                w_raw[first_chunk + i, k] = t[:, :, i * CHUNK:(i + 1) * CHUNK]
+
+        def load_cw(g):
+            t = ring("cw", GROUPS, g, [P, GROUP], BF16)
+            nc.sync.dma_start(out=t[:], in_=class_w[g * GROUP:(g + 1) * GROUP].partition_broadcast(P))
+            cw[g] = t
+
+        def turn_h(m, b):
+            t = bank(4 + (m * H_BANKS + b) % 4)
+            for g2 in range(2):
+                for u in range(2):
+                    col = (2 * g2 + u) * P
+                    nc.tensor.transpose(t[:, col:col + P], h_raw[m, b][:, 2 * P * g2 + u:2 * P * (g2 + 1):2], ident[:])
+            h_banks[m, b] = t
+
+        def group_h(m, b):
+            t = ring("hgr", 4, m * H_BANKS + b, [P, 2 * K_PASS], BF16)
+            nc.scalar.copy(
+                out=t[:].bitcast(F32).rearrange("p (g r u) -> p g r u", g=2, u=2),
+                in_=h_banks[m, b][:].rearrange("p (g u r) -> p g r u", g=2, u=2),
+            )
+            h_grouped[m, b] = t
+
+        def quantize_h(m, b):
+            if b == 0:
+                h_codes[m] = ring("hq", M_TILES, m, [P, PASSES * P], U32)
+                h_scales[m] = ring("hsc", M_TILES, m, [P, PASSES * P], U8)
+            cols = slice(2 * P * b, 2 * P * (b + 1))
+            nc.vector.quantize_mx(out=h_codes[m][:, cols].bitcast(FP8X4), scales=h_scales[m][:, cols], in_=h_grouped[m, b][:])
+
+        def group_w(c, k, engine):
+            t = ring("wgr", 5, c * PASSES + k, [P, CHUNK * PACK], BF16)
+            copy_on(
+                engine,
+                t[:].rearrange("p (c i t) -> p c t i", i=4, t=PACK),
+                w_raw[c, k].rearrange("p t (c i) -> p c t i", i=4),
+            )
+            w_grouped[c, k] = t
+
+        def quantize_w(c, k):
+            if k == 0:
+                w_codes[c] = ring("wq", 3, c, [P, PASSES * CHUNK], U32)
+                w_scales[c] = ring("wsc", 3, c, [P, PASSES * CHUNK], U8)
+            cols = slice(k * CHUNK, (k + 1) * CHUNK)
+            nc.vector.quantize_mx(out=w_codes[c][:, cols].bitcast(FP8X4), scales=w_scales[c][:, cols], in_=w_grouped[c, k][:])
+
+        def multiply(c, m):
+            t = bank(m % 4 if c == 0 else (c * M_TILES + m - M_TILES) % 6)
+            for k in range(PASSES):
+                student = k < S_PASSES
+                mc = slice(k * P, (k + 1) * P)
+                vc = slice(k * CHUNK, (k + 1) * CHUNK)
+                nc.tensor.matmul_mx(
+                    out=t[:, 0:CHUNK] if student else t[:, CHUNK:2 * CHUNK],
+                    lhsT=h_codes[m][:, mc].bitcast(FP8X4),
+                    lhsT_scale=h_scales[m][:, mc],
+                    rhs=w_codes[c][:, vc].bitcast(FP8X4),
+                    rhs_scale=w_scales[c][:, vc],
+                    start=k in (0, S_PASSES),
+                    stop=k in (S_PASSES - 1, PASSES - 1),
+                )
+            logits[c, m] = t
+
+        batches = []
+        for c in range(CHUNKS):
+            for q in range(M_TILES // 2):
+                if c == CHUNKS - 1 and q == M_TILES // 2 - 1:
+                    batches.append((c, (2 * q,)))
+                    batches.append((c, (2 * q + 1,)))
+                else:
+                    batches.append((c, (2 * q, 2 * q + 1)))
+
+        def sigmoid(n, j):
+            c, ms = batches[n]
+            if j == 0:
+                probs[n] = ring("prob", 3, n, [P, len(ms), 2 * CHUNK], F32)
+            nc.scalar.activation(out=probs[n][:, j, :], in_=logits[c, ms[j]][:], func=SIGMOID)
+
+        def subtract(n):
+            c, ms = batches[n]
+            diffs[n] = ring("diff", 2, n, [P, len(ms), CHUNK], F32)
+            nc.vector.tensor_sub(out=diffs[n][:], in0=probs[n][:, :, 0:CHUNK], in1=probs[n][:, :, CHUNK:2 * CHUNK])
+
+        def y_part(n):
+            c, ms = batches[n]
+            j0 = ms[0] % 2
+            return ys[c // 2, ms[0] // 2][:, j0:j0 + len(ms), (c % 2) * CHUNK:(c % 2 + 1) * CHUNK]
+
+        def weigh(n):
+            c, ms = batches[n]
+            g, q = c // 2, ms[0] // 2
+            if c % 2 == 0:
+                ys[g, q] = ring("y", 8, g * 4 + q, [P, 2, GROUP], F32)
+            factor = cw[g][:, (c % 2) * CHUNK:(c % 2 + 1) * CHUNK].unsqueeze(1).to_broadcast([P, len(ms), CHUNK])
+            nc.vector.tensor_mul(out=y_part(n), in0=diffs[n][:], in1=factor)
+
+        def store_y(n):
+            c, ms = batches[n]
+            g, q = c // 2, ms[0] // 2
+            rows = out_0[ms[0] * P:(ms[-1] + 1) * P, :]
+            if g == GROUPS - 1:
+                nc.sync.dma_start(out=rows[:, c * CHUNK:(c + 1) * CHUNK].rearrange("(j p) v -> p j v", p=P), in_=y_part(n))
+            elif c % 2 == 1:
+                nc.sync.dma_start(out=rows[:, g * GROUP:(g + 1) * GROUP].rearrange("(j p) v -> p j v", p=P), in_=ys[g, q][:])
+
+        def round_y(n, engine):
+            c, ms = batches[n]
+            g, q = c // 2, ms[0] // 2
+            if c % 2 == 0:
+                y_pairs[g, q] = ring("ybf", 6, g * 4 + q, [P, 2, 2, P, 2], BF16)
+            j0 = ms[0] % 2
+            half = slice((c % 2) * (P // 2), (c % 2 + 1) * (P // 2))
+            copy_on(
+                engine,
+                y_pairs[g, q][:, j0:j0 + len(ms), :, half, :],
+                y_part(n).rearrange("m j (p u e) -> m j u p e", u=2, e=2),
+            )
+
+        def has_planes(n):
+            return 0 <= n < len(batches) and batches[n][0] % 2 == 1
+
+        def turn_y(n):
+            c, ms = batches[n]
+            words = y_pairs[c // 2, ms[0] // 2][:].rearrange("m j u p e -> m (j u p e)").bitcast(F32)
+            t = bank(6 + n % 2)
+            j0 = ms[0] % 2
+            for i in range(2 * len(ms)):
+                src = (2 * j0 + i) * P
+                nc.tensor.transpose(t[:, i * P:(i + 1) * P], words[:, src:src + P], ident[:])
+            y_banks[n] = t
+
+        def group_y(n):
+            c, ms = batches[n]
+            t = ring("ygr", 3, n, [P, len(ms) * P * PACK], BF16)
+            nc.scalar.copy(
+                out=t[:].bitcast(F32).rearrange("p (j m u) -> p j m u", m=P, u=2),
+                in_=y_banks[n][:, 0:2 * P * len(ms)].rearrange("p (j u m) -> p j m u", m=P, u=2),
+            )
+            y_grouped[n] = t
+
+        def quantize_y(n):
+            c, ms = batches[n]
+            g = c // 2
+            if ms[0] == 0:
+                y_codes[g] = ring("yq", GROUPS, g, [P, M], U32)
+                y_scales[g] = ring("ysc", GROUPS, g, [P, M], U8)
+            cols = slice(ms[0] * P, (ms[-1] + 1) * P)
+            nc.vector.quantize_mx(out=y_codes[g][:, cols].bitcast(FP8X4), scales=y_scales[g][:, cols], in_=y_grouped[n][:])
+
+        def store_planes(n):
+            c, ms = batches[n]
+            g = c // 2
+            last = ms[-1] == M_TILES - 1
+            words = out_1[g].rearrange("p m t -> p (m t)").bitcast(I32)
+            if g == GROUPS - 1:
+                cols = slice(ms[0] * P, (ms[-1] + 1) * P)
+                nc.sync.dma_start(out=words[:, cols], in_=y_codes[g][:, cols].bitcast(I32))
+            elif last:
+                nc.sync.dma_start(out=words, in_=y_codes[g][:].bitcast(I32))
+            if last:
+                for quad in range(4):
+                    queue = nc.scalar if g == GROUPS - 1 and quad % 2 == 0 else nc.sync
+                    queue.dma_start(
+                        out=out_2[g, 4 * quad:4 * quad + 4, :].bitcast(I32),
+                        in_=y_scales[g][32 * quad:32 * quad + 4, :].bitcast(I32),
+                    )
+
+        load_hs(0)
+        load_w(0, 0, 1, 0)
+        load_w(1, 0, 1, 1)
+        load_ht(0)
+        for k in range(S_PASSES, PASSES):
+            load_w(k, 0, 1, k)
+        load_h(1)
+        load_cw(0)
+        load_h(2)
+        load_w(0, 1, 1, PASSES)
+        load_h(3)
+        load_w(1, 1, 1, PASSES + 1)
+
+        turn_h(0, 0)
+        group_h(0, 0)
+        group_w(0, 0, "vector")
+        group_w(0, 1, "scalar")
+        quantize_h(0, 0)
+        quantize_w(0, 0)
+        turn_h(0, 1)
+        turn_h(0, 2)
+        group_h(0, 1)
+        group_h(0, 2)
+        quantize_w(0, 1)
+        group_w(0, 2, "vector")
+        quantize_h(0, 1)
+        quantize_w(0, 2)
+        group_w(0, 3, "scalar")
+        quantize_h(0, 2)
+        group_w(0, 4, "vector")
+        quantize_w(0, 3)
+        quantize_w(0, 4)
+        group_w(0, 5, "vector")
+        quantize_w(0, 5)
+        load_h(4)
+        load_w(2, 1, 1, PASSES + 2)
+
+        for m in range(M_TILES):
+            nxt = m + 1 < M_TILES
+            n = m // 2
+            k = m - 2
+            if nxt:
+                for b in range(H_BANKS):
+                    turn_h(m + 1, b)
+                    group_h(m + 1, b)
+            if m + 5 < M_TILES:
+                load_h(m + 5)
+                load_w(m + 3, 1, 1, PASSES + m + 3)
+            if m == 3:
+                load_cw(1)
+                for kk in range(PASSES):
+                    load_w(kk, 2, 2, kk)
+            multiply(0, m)
+            sigmoid(n, m % 2)
+            if k >= 0:
+                group_w(1, k, "vector")
+            if m % 2 == 0 and n >= 1:
+                subtract(n - 1)
+            if m % 2 == 1 and n >= 1:
+                weigh(n - 1)
+            if nxt:
+                quantize_h(m + 1, 0)
+            if k >= 0:
+                quantize_w(1, k)
+            if nxt:
+                quantize_h(m + 1, 1)
+            if m % 2 == 1 and n >= 1:
+                round_y(n - 1, "vector")
+            if nxt:
+                quantize_h(m + 1, 2)
+
+        pieces = {n: [] for n in range(len(batches) + 3)}
+        for c in range(2, CHUNKS):
+            slots = [4, 4, 5, 5, 6, 6] if c == 2 else [4 * c - 5 + s for s in (0, 0, 1, 2, 2, 3)]
+            on_scalar = (1, 4) if c % 2 == 0 else (1,)
+            for k in range(PASSES):
+                pieces[slots[k]].append((c, k, "scalar" if k in on_scalar else "vector"))
+        late_loads = {5: [0, 1], 6: [2, 3], 7: [4, 5]}
+
+        pending = []
+        for n in range(4, len(batches) + 3):
+            live = n < len(batches)
+            prev = n - 1 < len(batches)
+            mine = sorted(pieces[n], key=lambda piece: piece[2] == "scalar")
+            if live:
+                c, ms = batches[n]
+                for j in range(len(ms)):
+                    multiply(c, ms[j])
+            if has_planes(n - 2):
+                turn_y(n - 2)
+            if live:
+                sigmoid(n, 0)
+            if has_planes(n - 3):
+                group_y(n - 3)
+            if live and len(ms) == 2:
+                sigmoid(n, 1)
+            if prev:
+                subtract(n - 1)
+            for cc, k in pending:
+                quantize_w(cc, k)
+            pending = []
+            on_vector = [piece for piece in mine if piece[2] == "vector"]
+            for cc, k, engine in on_vector[:1]:
+                group_w(cc, k, engine)
+            if prev:
+                weigh(n - 1)
+                store_y(n - 1)
+            for cc, k, engine in on_vector[:1]:
+                quantize_w(cc, k)
+            for cc, k, engine in on_vector[1:]:
+                group_w(cc, k, engine)
+            if has_planes(n - 3):
+                quantize_y(n - 3)
+                store_planes(n - 3)
+            if prev:
+                round_y(n - 1, "scalar" if n < 19 else "vector")
+            for cc, k, engine in on_vector[1:]:
+                quantize_w(cc, k)
+            for cc, k, engine in mine:
+                if engine == "scalar":
+                    group_w(cc, k, engine)
+                    pending.append((cc, k))
+            if n == 5:
+                load_cw(2)
+            for k in late_loads.get(n, []):
+                load_w(k, 4, 2, PASSES + k)

@@ -59,28 +59,24 @@ def tile_distill_logit_grad_g1_kernel(tc, h_student, w_student, h_teacher, w_tea
         logits, probs, diffs, ys, y_pairs, y_banks, y_grouped, y_codes, y_scales = {}, {}, {}, {}, {}, {}, {}, {}, {}
 
         def load_hs(m):
-            t = ring("hs", 4, m, [P, DS], BF16)
+            t = ring("ybf", 6, m, [P, DS], BF16) if m < 6 else ring("hs", 2, m, [P, DS], BF16)
             nc.sync.dma_start(out=t[:], in_=h_student[m * P:(m + 1) * P, :])
             h_raw[m, 0] = t[:].bitcast(F32)
 
         def load_ht(m):
-            t = ring("ht", 4, m, [P, DT], BF16)
+            t = ring("ht", 4, m, [P, DT], BF16) if m < 4 else ring("y", 8, m, [P, DT], BF16)
             nc.sync.dma_start(out=t[:], in_=h_teacher[m * P:(m + 1) * P, :])
             words = t[:].bitcast(F32)
             h_raw[m, 1] = words[:, 0:BANK]
             h_raw[m, 2] = words[:, BANK:2 * BANK]
 
-        def load_h(m):
-            load_hs(m)
-            load_ht(m)
-
-        def load_w(k, first_chunk, chunks, slot):
-            rows = w_student[k * K_PASS:(k + 1) * K_PASS, :] if k < S_PASSES else w_teacher[(k - S_PASSES) * K_PASS:(k - S_PASSES + 1) * K_PASS, :]
-            cols = slice(first_chunk * CHUNK, (first_chunk + chunks) * CHUNK)
-            t = ring("wraw", 2 * PASSES, slot, [P, PACK, chunks * CHUNK], BF16)
-            nc.sync.dma_start(out=t[:], in_=rows[:, cols].rearrange("(p j) c -> p j c", j=PACK))
-            for i in range(chunks):
-                w_raw[first_chunk + i, k] = t[:, :, i * CHUNK:(i + 1) * CHUNK]
+        def load_w(g, k):
+            source, row = (w_student, k) if k < S_PASSES else (w_teacher, k - S_PASSES)
+            rows = source[row * K_PASS:(row + 1) * K_PASS, g * GROUP:(g + 1) * GROUP]
+            t = ring("wraw", 10, g * PASSES + k, [P, PACK, GROUP], BF16)
+            nc.sync.dma_start(out=t[:], in_=rows.rearrange("(p j) c -> p j c", j=PACK))
+            for i in range(2):
+                w_raw[2 * g + i, k] = t[:, :, i * CHUNK:(i + 1) * CHUNK]
 
         def load_cw(g):
             t = ring("cw", GROUPS, g, [P, GROUP], BF16)
@@ -88,7 +84,7 @@ def tile_distill_logit_grad_g1_kernel(tc, h_student, w_student, h_teacher, w_tea
             cw[g] = t
 
         def turn_h(m, b):
-            t = bank(4 + (m * H_BANKS + b) % 4)
+            t = bank(len(h_banks) % 3)
             for g2 in range(2):
                 for u in range(2):
                     col = (2 * g2 + u) * P
@@ -96,7 +92,7 @@ def tile_distill_logit_grad_g1_kernel(tc, h_student, w_student, h_teacher, w_tea
             h_banks[m, b] = t
 
         def group_h(m, b):
-            t = ring("hgr", 4, m * H_BANKS + b, [P, 2 * K_PASS], BF16)
+            t = ring("hgr", 4, len(h_grouped), [P, 2 * K_PASS], BF16)
             nc.scalar.copy(
                 out=t[:].bitcast(F32).rearrange("p (g r u) -> p g r u", g=2, u=2),
                 in_=h_banks[m, b][:].rearrange("p (g u r) -> p g r u", g=2, u=2),
@@ -111,7 +107,7 @@ def tile_distill_logit_grad_g1_kernel(tc, h_student, w_student, h_teacher, w_tea
             nc.vector.quantize_mx(out=h_codes[m][:, cols].bitcast(FP8X4), scales=h_scales[m][:, cols], in_=h_grouped[m, b][:])
 
         def group_w(c, k, engine):
-            t = ring("wgr", 5, c * PASSES + k, [P, CHUNK * PACK], BF16)
+            t = ring("wgr", 5, len(w_grouped), [P, CHUNK * PACK], BF16)
             copy_on(
                 engine,
                 t[:].rearrange("p (c i t) -> p c t i", i=4, t=PACK),
@@ -120,118 +116,134 @@ def tile_distill_logit_grad_g1_kernel(tc, h_student, w_student, h_teacher, w_tea
             w_grouped[c, k] = t
 
         def quantize_w(c, k):
-            if k == 0:
-                w_codes[c] = ring("wq", 3, c, [P, PASSES * CHUNK], U32)
-                w_scales[c] = ring("wsc", 3, c, [P, PASSES * CHUNK], U8)
+            if c not in w_codes:
+                w_codes[c] = ring("wq", 4, c, [P, PASSES * CHUNK], U32)
+                w_scales[c] = ring("wsc", 4, c, [P, PASSES * CHUNK], U8)
             cols = slice(k * CHUNK, (k + 1) * CHUNK)
             nc.vector.quantize_mx(out=w_codes[c][:, cols].bitcast(FP8X4), scales=w_scales[c][:, cols], in_=w_grouped[c, k][:])
 
-        def multiply(c, m):
-            t = bank(m % 4 if c == 0 else (c * M_TILES + m - M_TILES) % 6)
-            for k in range(PASSES):
-                student = k < S_PASSES
+        def mx_group(out, c, m, passes):
+            for k in passes:
                 mc = slice(k * P, (k + 1) * P)
                 vc = slice(k * CHUNK, (k + 1) * CHUNK)
                 nc.tensor.matmul_mx(
-                    out=t[:, 0:CHUNK] if student else t[:, CHUNK:2 * CHUNK],
+                    out=out,
                     lhsT=h_codes[m][:, mc].bitcast(FP8X4),
                     lhsT_scale=h_scales[m][:, mc],
                     rhs=w_codes[c][:, vc].bitcast(FP8X4),
                     rhs_scale=w_scales[c][:, vc],
-                    start=k in (0, S_PASSES),
-                    stop=k in (S_PASSES - 1, PASSES - 1),
+                    start=k == passes[0],
+                    stop=k == passes[-1],
                 )
+
+        student, teacher = range(S_PASSES), range(S_PASSES, PASSES)
+
+        def multiply_first(m, passes):
+            t = bank(3 + m % 3 if passes == student else 3 + (M_TILES + m) % 3)
+            mx_group(t[:, 0:CHUNK], 0, m, passes)
+            mx_group(t[:, CHUNK:2 * CHUNK], 1, m, passes)
+            logits[0, m] = t
+
+        def multiply(c, m):
+            t = bank((c * M_TILES + m) % 6)
+            mx_group(t[:, 0:CHUNK], c, m, student)
+            mx_group(t[:, CHUNK:2 * CHUNK], c, m, teacher)
             logits[c, m] = t
 
-        batches = []
-        for c in range(CHUNKS):
+        batches = [(0, (m,), 0, GROUP) for m in range(M_TILES)]
+        for c in range(2, CHUNKS):
             for q in range(M_TILES // 2):
                 if c == CHUNKS - 1 and q == M_TILES // 2 - 1:
-                    batches.append((c, (2 * q,)))
-                    batches.append((c, (2 * q + 1,)))
+                    batches.append((c // 2, (2 * q,), CHUNK, CHUNK))
+                    batches.append((c // 2, (2 * q + 1,), CHUNK, CHUNK))
                 else:
-                    batches.append((c, (2 * q, 2 * q + 1)))
+                    batches.append((c // 2, (2 * q, 2 * q + 1), (c % 2) * CHUNK, CHUNK))
+
+        def y_part(n):
+            g, ms, col, width = batches[n]
+            j0 = ms[0] % 2
+            return ys[g, ms[0] // 2][:, j0:j0 + len(ms), col:col + width]
+
+        def new_y(g, q):
+            ys[g, q] = ring("y", 8, g * 4 + q, [P, 2, GROUP], F32)
+
+        def sigmoid_student(m):
+            if m % 2 == 0:
+                new_y(0, m // 2)
+            nc.scalar.activation(out=ys[0, m // 2][:, m % 2, :], in_=logits[0, m][:], func=SIGMOID)
 
         def sigmoid(n, j):
-            c, ms = batches[n]
+            g, ms, col, width = batches[n]
             if j == 0:
-                probs[n] = ring("prob", 3, n, [P, len(ms), 2 * CHUNK], F32)
+                probs[n] = ring("prob", 3, n, [P, len(ms), BANK], F32)
+            c = 0 if g == 0 else 2 * g + col // CHUNK
             nc.scalar.activation(out=probs[n][:, j, :], in_=logits[c, ms[j]][:], func=SIGMOID)
 
         def subtract(n):
-            c, ms = batches[n]
-            diffs[n] = ring("diff", 2, n, [P, len(ms), CHUNK], F32)
-            nc.vector.tensor_sub(out=diffs[n][:], in0=probs[n][:, :, 0:CHUNK], in1=probs[n][:, :, CHUNK:2 * CHUNK])
-
-        def y_part(n):
-            c, ms = batches[n]
-            j0 = ms[0] % 2
-            return ys[c // 2, ms[0] // 2][:, j0:j0 + len(ms), (c % 2) * CHUNK:(c % 2 + 1) * CHUNK]
+            g, ms, col, width = batches[n]
+            diffs[n] = ring("diff", 2, n, [P, len(ms), width], F32)
+            if g == 0:
+                nc.vector.tensor_sub(out=diffs[n][:], in0=y_part(n), in1=probs[n][:])
+            else:
+                nc.vector.tensor_sub(out=diffs[n][:], in0=probs[n][:, :, 0:CHUNK], in1=probs[n][:, :, CHUNK:2 * CHUNK])
 
         def weigh(n):
-            c, ms = batches[n]
-            g, q = c // 2, ms[0] // 2
-            if c % 2 == 0:
-                ys[g, q] = ring("y", 8, g * 4 + q, [P, 2, GROUP], F32)
-            factor = cw[g][:, (c % 2) * CHUNK:(c % 2 + 1) * CHUNK].unsqueeze(1).to_broadcast([P, len(ms), CHUNK])
+            g, ms, col, width = batches[n]
+            if g > 0 and col == 0:
+                new_y(g, ms[0] // 2)
+            factor = cw[g][:, col:col + width].unsqueeze(1).to_broadcast([P, len(ms), width])
             nc.vector.tensor_mul(out=y_part(n), in0=diffs[n][:], in1=factor)
 
         def store_y(n):
-            c, ms = batches[n]
-            g, q = c // 2, ms[0] // 2
-            rows = out_0[ms[0] * P:(ms[-1] + 1) * P, :]
+            g, ms, col, width = batches[n]
+            q = ms[0] // 2
             if g == GROUPS - 1:
-                nc.sync.dma_start(out=rows[:, c * CHUNK:(c + 1) * CHUNK].rearrange("(j p) v -> p j v", p=P), in_=y_part(n))
-            elif c % 2 == 1:
-                nc.sync.dma_start(out=rows[:, g * GROUP:(g + 1) * GROUP].rearrange("(j p) v -> p j v", p=P), in_=ys[g, q][:])
+                rows = out_0[ms[0] * P:(ms[-1] + 1) * P, g * GROUP + col:g * GROUP + col + width]
+                nc.sync.dma_start(out=rows.rearrange("(j p) v -> p j v", p=P), in_=y_part(n))
+            elif ms[-1] % 2 == 1 and col + width == GROUP:
+                rows = out_0[2 * q * P:(2 * q + 2) * P, g * GROUP:(g + 1) * GROUP]
+                nc.sync.dma_start(out=rows.rearrange("(j p) v -> p j v", p=P), in_=ys[g, q][:])
 
-        def round_y(n, engine):
-            c, ms = batches[n]
-            g, q = c // 2, ms[0] // 2
-            if c % 2 == 0:
+        units = [(g, (2 * q, 2 * q + 1)) for g in range(GROUPS) for q in range(M_TILES // 2)]
+        units = units[:-1] + [(GROUPS - 1, (m,)) for m in units[-1][1]]
+
+        def round_y(g, ms, col, width, engine):
+            j0, q = ms[0] % 2, ms[0] // 2
+            if j0 == 0 and col == 0:
                 y_pairs[g, q] = ring("ybf", 6, g * 4 + q, [P, 2, 2, P, 2], BF16)
-            j0 = ms[0] % 2
-            half = slice((c % 2) * (P // 2), (c % 2 + 1) * (P // 2))
             copy_on(
                 engine,
-                y_pairs[g, q][:, j0:j0 + len(ms), :, half, :],
-                y_part(n).rearrange("m j (p u e) -> m j u p e", u=2, e=2),
+                y_pairs[g, q][:, j0:j0 + len(ms), :, col // PACK:(col + width) // PACK, :],
+                ys[g, q][:, j0:j0 + len(ms), col:col + width].rearrange("m j (p u e) -> m j u p e", u=2, e=2),
             )
 
-        def has_planes(n):
-            return 0 <= n < len(batches) and batches[n][0] % 2 == 1
-
-        def turn_y(n):
-            c, ms = batches[n]
-            words = y_pairs[c // 2, ms[0] // 2][:].rearrange("m j u p e -> m (j u p e)").bitcast(F32)
-            t = bank(6 + n % 2)
-            j0 = ms[0] % 2
+        def turn_y(u):
+            g, ms = units[u]
+            words = y_pairs[g, ms[0] // 2][:].rearrange("m j u p e -> m (j u p e)").bitcast(F32)
+            y_banks[u] = bank(6 + u % 2 if u < 10 else u - 10)
             for i in range(2 * len(ms)):
-                src = (2 * j0 + i) * P
-                nc.tensor.transpose(t[:, i * P:(i + 1) * P], words[:, src:src + P], ident[:])
-            y_banks[n] = t
+                src = (2 * (ms[0] % 2) + i) * P
+                nc.tensor.transpose(y_banks[u][:, i * P:(i + 1) * P], words[:, src:src + P], ident[:])
 
-        def group_y(n):
-            c, ms = batches[n]
-            t = ring("ygr", 3, n, [P, len(ms) * P * PACK], BF16)
+        def group_y(u):
+            g, ms = units[u]
+            t = ring("ygr", 3, u, [P, len(ms) * P * PACK], BF16)
             nc.scalar.copy(
                 out=t[:].bitcast(F32).rearrange("p (j m u) -> p j m u", m=P, u=2),
-                in_=y_banks[n][:, 0:2 * P * len(ms)].rearrange("p (j u m) -> p j m u", m=P, u=2),
+                in_=y_banks[u][:, 0:2 * P * len(ms)].rearrange("p (j u m) -> p j m u", m=P, u=2),
             )
-            y_grouped[n] = t
+            y_grouped[u] = t
 
-        def quantize_y(n):
-            c, ms = batches[n]
-            g = c // 2
+        def quantize_y(u):
+            g, ms = units[u]
             if ms[0] == 0:
                 y_codes[g] = ring("yq", GROUPS, g, [P, M], U32)
                 y_scales[g] = ring("ysc", GROUPS, g, [P, M], U8)
             cols = slice(ms[0] * P, (ms[-1] + 1) * P)
-            nc.vector.quantize_mx(out=y_codes[g][:, cols].bitcast(FP8X4), scales=y_scales[g][:, cols], in_=y_grouped[n][:])
+            nc.vector.quantize_mx(out=y_codes[g][:, cols].bitcast(FP8X4), scales=y_scales[g][:, cols], in_=y_grouped[u][:])
 
-        def store_planes(n):
-            c, ms = batches[n]
-            g = c // 2
+        def store_planes(u):
+            g, ms = units[u]
             last = ms[-1] == M_TILES - 1
             words = out_1[g].rearrange("p m t -> p (m t)").bitcast(I32)
             if g == GROUPS - 1:
@@ -248,128 +260,122 @@ def tile_distill_logit_grad_g1_kernel(tc, h_student, w_student, h_teacher, w_tea
                     )
 
         load_hs(0)
-        load_w(0, 0, 1, 0)
-        load_w(1, 0, 1, 1)
+        load_w(0, 0)
+        load_hs(1)
+        load_w(0, 1)
+        for s in range(1, M_TILES // 2):
+            load_hs(2 * s)
+            load_hs(2 * s + 1)
+            load_w(0, S_PASSES + s - 1)
         load_ht(0)
-        for k in range(S_PASSES, PASSES):
-            load_w(k, 0, 1, k)
-        load_h(1)
+        load_w(0, PASSES - 1)
+        load_ht(1)
         load_cw(0)
-        load_h(2)
-        load_w(0, 1, 1, PASSES)
-        load_h(3)
-        load_w(1, 1, 1, PASSES + 1)
+        load_ht(2)
 
         turn_h(0, 0)
         group_h(0, 0)
+        turn_h(1, 0)
         group_w(0, 0, "vector")
-        group_w(0, 1, "scalar")
+        group_w(1, 0, "scalar")
         quantize_h(0, 0)
         quantize_w(0, 0)
-        turn_h(0, 1)
-        turn_h(0, 2)
-        group_h(0, 1)
-        group_h(0, 2)
+        group_h(1, 0)
+        group_w(0, 1, "vector")
+        quantize_w(1, 0)
+        group_w(1, 1, "scalar")
+        quantize_h(1, 0)
         quantize_w(0, 1)
-        group_w(0, 2, "vector")
-        quantize_h(0, 1)
-        quantize_w(0, 2)
-        group_w(0, 3, "scalar")
-        quantize_h(0, 2)
-        group_w(0, 4, "vector")
-        quantize_w(0, 3)
-        quantize_w(0, 4)
-        group_w(0, 5, "vector")
-        quantize_w(0, 5)
-        load_h(4)
-        load_w(2, 1, 1, PASSES + 2)
-
+        quantize_w(1, 1)
         for m in range(M_TILES):
-            nxt = m + 1 < M_TILES
-            n = m // 2
-            k = m - 2
-            if nxt:
-                for b in range(H_BANKS):
-                    turn_h(m + 1, b)
-                    group_h(m + 1, b)
-            if m + 5 < M_TILES:
-                load_h(m + 5)
-                load_w(m + 3, 1, 1, PASSES + m + 3)
-            if m == 3:
-                load_cw(1)
-                for kk in range(PASSES):
-                    load_w(kk, 2, 2, kk)
-            multiply(0, m)
-            sigmoid(n, m % 2)
-            if k >= 0:
-                group_w(1, k, "vector")
-            if m % 2 == 0 and n >= 1:
-                subtract(n - 1)
-            if m % 2 == 1 and n >= 1:
-                weigh(n - 1)
-            if nxt:
-                quantize_h(m + 1, 0)
-            if k >= 0:
-                quantize_w(1, k)
-            if nxt:
-                quantize_h(m + 1, 1)
-            if m % 2 == 1 and n >= 1:
-                round_y(n - 1, "vector")
-            if nxt:
-                quantize_h(m + 1, 2)
+            ahead = [(m + 2, 0)] if m + 2 < M_TILES else [(m + 2 - M_TILES, 1), (m + 2 - M_TILES, 2)]
+            for mm, b in ahead:
+                turn_h(mm, b)
+                group_h(mm, b)
+            multiply_first(m, student)
+            sigmoid_student(m)
+            c, k = m % 2, S_PASSES + m // 2
+            group_w(c, k, "vector")
+            quantize_h(*ahead[0])
+            quantize_w(c, k)
+            for mm, b in ahead[1:]:
+                quantize_h(mm, b)
 
-        pieces = {n: [] for n in range(len(batches) + 3)}
-        for c in range(2, CHUNKS):
-            slots = [4, 4, 5, 5, 6, 6] if c == 2 else [4 * c - 5 + s for s in (0, 0, 1, 2, 2, 3)]
-            on_scalar = (1, 4) if c % 2 == 0 else (1,)
-            for k in range(PASSES):
-                pieces[slots[k]].append((c, k, "scalar" if k in on_scalar else "vector"))
-        late_loads = {5: [0, 1], 6: [2, 3], 7: [4, 5]}
+        steps = range(len(batches) + 4)
+        pieces = {n: [] for n in steps}
+        for n, c, k, engine in [(1, 2, 0, "scalar"), (2, 2, 1, "scalar"), (2, 3, 0, "vector"), (3, 2, 2, "scalar"), (3, 3, 1, "vector"), (4, 2, 3, "scalar"), (5, 2, 4, "scalar"), (5, 3, 2, "vector"), (6, 2, 5, "vector"), (6, 3, 3, "scalar"), (7, 3, 4, "scalar"), (7, 3, 5, "vector"), (8, 4, 0, "vector"), (9, 4, 1, "scalar"), (10, 4, 2, "vector"), (11, 4, 3, "scalar"), (12, 4, 4, "scalar"), (13, 4, 5, "vector"), (13, 5, 0, "scalar"), (14, 5, 1, "vector"), (15, 5, 2, "scalar"), (15, 5, 3, "vector"), (16, 5, 4, "scalar"), (17, 5, 5, "vector")]:
+            pieces[n].append((c, k, engine))
+        loads = {0: [(1, 0)], 1: [(1, 1)], 2: [(1, 2)], 3: [(1, 3)], 4: [(1, 4), (1, 5), (2, 0), (2, 1), (2, 2), (2, 3), (2, 4), (2, 5)]}
+        rounds = {n: [] for n in steps}
+        turns = {}
+        for u, (g, ms) in enumerate(units):
+            if g < GROUPS - 1:
+                n = [8, 10, 12, 14, 16, 18, 19, 20][u]
+                rounds[n].append((g, ms, 0, GROUP, ["vector", "vector", "vector", "vector", "vector", "vector", "scalar", "scalar"][u]))
+                turns[n + 2] = u
+        for n, batch in enumerate(batches):
+            if batch[0] == GROUPS - 1:
+                rounds[n + 2].append(batch + ("vector",))
+                if batch[2] > 0:
+                    turns[n + 3] = units.index(batch[:2])
 
         pending = []
-        for n in range(4, len(batches) + 3):
+        for n in steps:
             live = n < len(batches)
-            prev = n - 1 < len(batches)
-            mine = sorted(pieces[n], key=lambda piece: piece[2] == "scalar")
-            if live:
-                c, ms = batches[n]
-                for j in range(len(ms)):
-                    multiply(c, ms[j])
-            if has_planes(n - 2):
-                turn_y(n - 2)
+            group = [1, 2] if n + 2 < M_TILES else []
+            for b in group:
+                turn_h(n + 2, b)
+                group_h(n + 2, b)
+            if n < M_TILES:
+                multiply_first(n, teacher)
+            elif live:
+                g, ms, col, width = batches[n]
+                for m in ms:
+                    multiply(2 * g + col // CHUNK, m)
+            if n in turns:
+                turn_y(turns[n])
             if live:
                 sigmoid(n, 0)
-            if has_planes(n - 3):
-                group_y(n - 3)
-            if live and len(ms) == 2:
+            if n - 1 in turns:
+                group_y(turns[n - 1])
+            if live and len(batches[n][1]) == 2:
                 sigmoid(n, 1)
-            if prev:
+            if n + 3 < M_TILES:
+                load_ht(n + 3)
+            on_vector = [piece for piece in pieces[n] if piece[2] == "vector"]
+            if 0 <= n - 1 < len(batches):
                 subtract(n - 1)
+            for task in rounds[n]:
+                round_y(*task)
+            for cc, k, engine in on_vector[:1]:
+                group_w(cc, k, engine)
+            for b in group[:1]:
+                quantize_h(n + 2, b)
+            if 0 <= n - 1 < len(batches):
+                weigh(n - 1)
+                if n - 1 >= M_TILES:
+                    store_y(n - 1)
+                if 8 <= n < 8 + 4:
+                    store_y(2 * (n - 8) + 1)
+            for cc, k, engine in on_vector[:1]:
+                quantize_w(cc, k)
+            for cc, k, engine in on_vector[1:]:
+                group_w(cc, k, engine)
             for cc, k in pending:
                 quantize_w(cc, k)
             pending = []
-            on_vector = [piece for piece in mine if piece[2] == "vector"]
-            for cc, k, engine in on_vector[:1]:
-                group_w(cc, k, engine)
-            if prev:
-                weigh(n - 1)
-                store_y(n - 1)
-            for cc, k, engine in on_vector[:1]:
-                quantize_w(cc, k)
-            for cc, k, engine in on_vector[1:]:
-                group_w(cc, k, engine)
-            if has_planes(n - 3):
-                quantize_y(n - 3)
-                store_planes(n - 3)
-            if prev:
-                round_y(n - 1, "scalar" if n < 19 else "vector")
+            if n - 1 in turns:
+                quantize_y(turns[n - 1])
+                store_planes(turns[n - 1])
+            for b in group[1:]:
+                quantize_h(n + 2, b)
             for cc, k, engine in on_vector[1:]:
                 quantize_w(cc, k)
-            for cc, k, engine in mine:
+            for cc, k, engine in pieces[n]:
                 if engine == "scalar":
                     group_w(cc, k, engine)
                     pending.append((cc, k))
-            if n == 5:
-                load_cw(2)
-            for k in late_loads.get(n, []):
-                load_w(k, 4, 2, PASSES + k)
+            for g, k in loads.get(n, []):
+                if k == 0:
+                    load_cw(g)
+                load_w(g, k)

@@ -26,6 +26,7 @@ GROUP = 512
 GROUPS = V // GROUP
 BANK = 512
 H_BANKS = PASSES // 2
+EARLY = 5
 
 
 def tile_distill_logit_grad_g1_kernel(tc, h_student, w_student, h_teacher, w_teacher, class_w, out_0, out_1, out_2):
@@ -73,15 +74,26 @@ def tile_distill_logit_grad_g1_kernel(tc, h_student, w_student, h_teacher, w_tea
         def load_w(g, k):
             source, row = (w_student, k) if k < S_PASSES else (w_teacher, k - S_PASSES)
             rows = source[row * K_PASS:(row + 1) * K_PASS, g * GROUP:(g + 1) * GROUP]
-            t = ring("wraw", 10, g * PASSES + k, [P, PACK, GROUP], BF16)
+            t = ring("wraw", 8, g * PASSES + k, [P, PACK, GROUP], BF16)
             nc.sync.dma_start(out=t[:], in_=rows.rearrange("(p j) c -> p j c", j=PACK))
             for i in range(2):
                 w_raw[2 * g + i, k] = t[:, :, i * CHUNK:(i + 1) * CHUNK]
 
-        def load_cw(g):
-            t = ring("cw", GROUPS, g, [P, GROUP], BF16)
-            nc.sync.dma_start(out=t[:], in_=class_w[g * GROUP:(g + 1) * GROUP].partition_broadcast(P))
-            cw[g] = t
+        def spread_class_w():
+            spread = sb.tile([P, V], BF16, name="cw")
+            words = class_w.bitcast(F32)
+            for part, (first, per) in enumerate(((0, 4), (4 * P, 2))):
+                column = sb.tile([P, per], F32, name="cw_column", tag="cw_column%d" % part)
+                nc.sync.dma_start(out=column[:], in_=words[first:first + per * P].rearrange("(p c) -> p c", c=per))
+                t = bank(6 + part)
+                for c in range(per):
+                    nc.tensor.transpose(t[:, c * P:(c + 1) * P], column[:, c:c + 1].to_broadcast([P, P]), ident[:])
+                nc.vector.tensor_copy(
+                    out=spread[:].bitcast(F32)[:, first:first + per * P].rearrange("q (p c) -> q p c", c=per),
+                    in_=t[:, 0:per * P].rearrange("q (c p) -> q p c", p=P),
+                )
+            for g in range(GROUPS):
+                cw[g] = spread[:, g * GROUP:(g + 1) * GROUP]
 
         def turn_h(m, b):
             t = bank(len(h_banks) % 3)
@@ -117,8 +129,8 @@ def tile_distill_logit_grad_g1_kernel(tc, h_student, w_student, h_teacher, w_tea
 
         def quantize_w(c, k):
             if c not in w_codes:
-                w_codes[c] = ring("wq", 4, c, [P, PASSES * CHUNK], U32)
-                w_scales[c] = ring("wsc", 4, c, [P, PASSES * CHUNK], U8)
+                w_codes[c] = ring("wq", CHUNKS, c, [P, PASSES * CHUNK], U32)
+                w_scales[c] = ring("wsc", CHUNKS, c, [P, PASSES * CHUNK], U8)
             cols = slice(k * CHUNK, (k + 1) * CHUNK)
             nc.vector.quantize_mx(out=w_codes[c][:, cols].bitcast(FP8X4), scales=w_scales[c][:, cols], in_=w_grouped[c, k][:])
 
@@ -225,12 +237,13 @@ def tile_distill_logit_grad_g1_kernel(tc, h_student, w_student, h_teacher, w_tea
                 src = (2 * (ms[0] % 2) + i) * P
                 nc.tensor.transpose(y_banks[u][:, i * P:(i + 1) * P], words[:, src:src + P], ident[:])
 
-        def group_y(u):
+        def group_y(u, engine):
             g, ms = units[u]
             t = ring("ygr", 3, u, [P, len(ms) * P * PACK], BF16)
-            nc.scalar.copy(
-                out=t[:].bitcast(F32).rearrange("p (j m u) -> p j m u", m=P, u=2),
-                in_=y_banks[u][:, 0:2 * P * len(ms)].rearrange("p (j u m) -> p j m u", m=P, u=2),
+            copy_on(
+                engine,
+                t[:].bitcast(F32).rearrange("p (j m u) -> p j m u", m=P, u=2),
+                y_banks[u][:, 0:2 * P * len(ms)].rearrange("p (j u m) -> p j m u", m=P, u=2),
             )
             y_grouped[u] = t
 
@@ -247,8 +260,9 @@ def tile_distill_logit_grad_g1_kernel(tc, h_student, w_student, h_teacher, w_tea
             last = ms[-1] == M_TILES - 1
             words = out_1[g].rearrange("p m t -> p (m t)").bitcast(I32)
             if g == GROUPS - 1:
-                cols = slice(ms[0] * P, (ms[-1] + 1) * P)
-                nc.sync.dma_start(out=words[:, cols], in_=y_codes[g][:, cols].bitcast(I32))
+                if ms[-1] in {3: 0, 5: 4, 7: 6}:
+                    cols = slice({3: 0, 5: 4, 7: 6}[ms[-1]] * P, (ms[-1] + 1) * P)
+                    nc.sync.dma_start(out=words[:, cols], in_=y_codes[g][:, cols].bitcast(I32))
             elif last:
                 nc.sync.dma_start(out=words, in_=y_codes[g][:].bitcast(I32))
             if last:
@@ -259,10 +273,13 @@ def tile_distill_logit_grad_g1_kernel(tc, h_student, w_student, h_teacher, w_tea
                         in_=y_scales[g][32 * quad:32 * quad + 4, :].bitcast(I32),
                     )
 
+        spread_class_w()
         load_hs(0)
         load_w(0, 0)
-        load_hs(1)
         load_w(0, 1)
+        load_hs(1)
+        turn_h(0, 0)
+        group_h(0, 0)
         for s in range(1, M_TILES // 2):
             load_hs(2 * s)
             load_hs(2 * s + 1)
@@ -270,23 +287,20 @@ def tile_distill_logit_grad_g1_kernel(tc, h_student, w_student, h_teacher, w_tea
         load_ht(0)
         load_w(0, PASSES - 1)
         load_ht(1)
-        load_cw(0)
-        load_ht(2)
+        load_w(1, 0)
 
-        turn_h(0, 0)
-        group_h(0, 0)
-        turn_h(1, 0)
         group_w(0, 0, "vector")
         group_w(1, 0, "scalar")
         quantize_h(0, 0)
         quantize_w(0, 0)
-        group_h(1, 0)
         group_w(0, 1, "vector")
         quantize_w(1, 0)
         group_w(1, 1, "scalar")
-        quantize_h(1, 0)
+        turn_h(1, 0)
+        group_h(1, 0)
         quantize_w(0, 1)
         quantize_w(1, 1)
+        quantize_h(1, 0)
         for m in range(M_TILES):
             ahead = [(m + 2, 0)] if m + 2 < M_TILES else [(m + 2 - M_TILES, 1), (m + 2 - M_TILES, 2)]
             for mm, b in ahead:
@@ -301,28 +315,35 @@ def tile_distill_logit_grad_g1_kernel(tc, h_student, w_student, h_teacher, w_tea
             for mm, b in ahead[1:]:
                 quantize_h(mm, b)
 
-        steps = range(len(batches) + 4)
+
+        steps = range(len(batches) + 5)
         pieces = {n: [] for n in steps}
-        for n, c, k, engine in [(1, 2, 0, "scalar"), (2, 2, 1, "scalar"), (2, 3, 0, "vector"), (3, 2, 2, "scalar"), (3, 3, 1, "vector"), (4, 2, 3, "scalar"), (5, 2, 4, "scalar"), (5, 3, 2, "vector"), (6, 2, 5, "vector"), (6, 3, 3, "scalar"), (7, 3, 4, "scalar"), (7, 3, 5, "vector"), (8, 4, 0, "vector"), (9, 4, 1, "scalar"), (10, 4, 2, "vector"), (11, 4, 3, "scalar"), (12, 4, 4, "scalar"), (13, 4, 5, "vector"), (13, 5, 0, "scalar"), (14, 5, 1, "vector"), (15, 5, 2, "scalar"), (15, 5, 3, "vector"), (16, 5, 4, "scalar"), (17, 5, 5, "vector")]:
+        for n, c, k, engine in [(0, 2, 0, "scalar"), (0, 3, 0, "vector"), (1, 2, 1, "scalar"), (1, 3, 1, "vector"), (2, 2, 2, "scalar"), (2, 3, 2, "vector"), (3, 2, 3, "scalar"), (3, 3, 3, "vector"), (4, 2, 4, "scalar"), (4, 3, 4, "vector"), (5, 2, 5, "scalar"), (5, 3, 5, "vector"), (6, 4, 0, "scalar"), (7, 4, 1, "scalar"), (8, 4, 2, "vector"), (9, 4, 3, "scalar"), (10, 4, 4, "scalar"), (11, 4, 5, "vector"), (12, 5, 0, "scalar"), (13, 5, 1, "scalar"), (14, 5, 2, "vector"), (15, 5, 3, "scalar"), (16, 5, 4, "scalar"), (17, 5, 5, "vector")]:
             pieces[n].append((c, k, engine))
-        loads = {0: [(1, 0)], 1: [(1, 1)], 2: [(1, 2)], 3: [(1, 3)], 4: [(1, 4), (1, 5), (2, 0), (2, 1), (2, 2), (2, 3), (2, 4), (2, 5)]}
+        loads = {0: [(1, 1)], 1: [(1, 2)], 2: [(1, 3)], 3: [(1, 4)], 4: [(1, 5)], 5: [(2, 0), (2, 1), (2, 2), (2, 3), (2, 4), (2, 5)]}
         rounds = {n: [] for n in steps}
-        turns = {}
+        turns = {n: [] for n in steps}
+        groups = {n: [] for n in steps}
         for u, (g, ms) in enumerate(units):
             if g < GROUPS - 1:
-                n = [8, 10, 12, 14, 16, 18, 19, 20][u]
-                rounds[n].append((g, ms, 0, GROUP, ["vector", "vector", "vector", "vector", "vector", "vector", "scalar", "scalar"][u]))
-                turns[n + 2] = u
+                n = [8, 9, 11, 12, 14, 15, 17, 18][u]
+                rounds[n].append((g, ms, 0, GROUP, (["vector"] * 8)[u]))
+                turns[[11, 11, 14, 14, 17, 17, 20, 20][u]].append(u)
+                groups[[12, 13, 15, 16, 18, 19, 21, 22][u]].append((u, "scalar"))
         for n, batch in enumerate(batches):
             if batch[0] == GROUPS - 1:
-                rounds[n + 2].append(batch + ("vector",))
+                rounds[n + 2].append(batch + ("scalar" if n in (20, 21, 22) else "vector",))
                 if batch[2] > 0:
-                    turns[n + 3] = units.index(batch[:2])
+                    u = units.index(batch[:2])
+                    turns[n + 4].append(u)
+                    groups[n + 4 + 1].append((u, "vector" if n in () else "scalar"))
 
         pending = []
         for n in steps:
             live = n < len(batches)
             group = [1, 2] if n + 2 < M_TILES else []
+            if group:
+                load_ht(n + 2)
             for b in group:
                 turn_h(n + 2, b)
                 group_h(n + 2, b)
@@ -332,50 +353,40 @@ def tile_distill_logit_grad_g1_kernel(tc, h_student, w_student, h_teacher, w_tea
                 g, ms, col, width = batches[n]
                 for m in ms:
                     multiply(2 * g + col // CHUNK, m)
-            if n in turns:
-                turn_y(turns[n])
+            for u in turns[n]:
+                turn_y(u)
             if live:
                 sigmoid(n, 0)
-            if n - 1 in turns:
-                group_y(turns[n - 1])
+            for u, engine in groups[n]:
+                group_y(u, engine)
             if live and len(batches[n][1]) == 2:
                 sigmoid(n, 1)
-            if n + 3 < M_TILES:
-                load_ht(n + 3)
             on_vector = [piece for piece in pieces[n] if piece[2] == "vector"]
+            fill = [lambda cc=cc, k=k: group_w(cc, k, "vector") for cc, k, engine in on_vector]
+            fill.extend([lambda task=task: round_y(*task) for task in rounds[n] if task[-1] == "vector"])
+            fill.extend([lambda cc=cc, k=k: quantize_w(cc, k) for cc, k in pending])
+            fill.extend([lambda u=u: (quantize_y(u), store_planes(u)) for u, engine in groups[n]])
+            fill.extend([lambda b=b: quantize_h(n + 2, b) for b in group])
+            fill.extend([lambda cc=cc, k=k: quantize_w(cc, k) for cc, k, engine in on_vector])
+            pending = []
             if 0 <= n - 1 < len(batches):
                 subtract(n - 1)
-            for task in rounds[n]:
-                round_y(*task)
-            for cc, k, engine in on_vector[:1]:
-                group_w(cc, k, engine)
-            for b in group[:1]:
-                quantize_h(n + 2, b)
+            for task in fill[:1]:
+                task()
             if 0 <= n - 1 < len(batches):
                 weigh(n - 1)
                 if n - 1 >= M_TILES:
                     store_y(n - 1)
                 if 8 <= n < 8 + 4:
                     store_y(2 * (n - 8) + 1)
-            for cc, k, engine in on_vector[:1]:
-                quantize_w(cc, k)
-            for cc, k, engine in on_vector[1:]:
-                group_w(cc, k, engine)
-            for cc, k in pending:
-                quantize_w(cc, k)
-            pending = []
-            if n - 1 in turns:
-                quantize_y(turns[n - 1])
-                store_planes(turns[n - 1])
-            for b in group[1:]:
-                quantize_h(n + 2, b)
-            for cc, k, engine in on_vector[1:]:
-                quantize_w(cc, k)
+            for task in fill[1:]:
+                task()
+            for task in rounds[n]:
+                if task[-1] == "scalar":
+                    round_y(*task)
             for cc, k, engine in pieces[n]:
                 if engine == "scalar":
                     group_w(cc, k, engine)
                     pending.append((cc, k))
             for g, k in loads.get(n, []):
-                if k == 0:
-                    load_cw(g)
                 load_w(g, k)

@@ -17,30 +17,41 @@ SIGMOID = mybir.ActivationFunctionType.Sigmoid
 P = 128
 PACK = 4
 K_PASS = P * PACK
-S_PASSES = DS // K_PASS
-PASSES = (DS + DT) // K_PASS
-M_TILES = M // P
-CHUNK = 256
-CHUNKS = V // CHUNK
-GROUP = 512
+STUDENT = range(DS // K_PASS)
+TEACHER = range(DS // K_PASS, (DS + DT) // K_PASS)
+PASSES = len(STUDENT) + len(TEACHER)
+TILES = M // P
+PAIRS = TILES // 2
+GROUP = K_PASS
 GROUPS = V // GROUP
+LAST = GROUPS - 1
+CHUNK = GROUP // 2
 BANK = 512
-H_BANKS = PASSES // 2
-EARLY = 5
 
 
-def tile_distill_logit_grad_g1_kernel(tc, h_student, w_student, h_teacher, w_teacher, class_w, out_0, out_1, out_2):
+def tile_distill_logit_grad_g1_kernel(
+    tc, h_student, w_student, h_teacher, w_teacher, class_w, out_0, out_1, out_2
+):
     nc = tc.nc
     with ExitStack() as ctx:
-        sb = ctx.enter_context(tc.tile_pool(name="sb", bufs=1))
-        ps = ctx.enter_context(tc.psum_pool(name="ps", bufs=1))
+        sbuf = ctx.enter_context(tc.tile_pool(name="sbuf", bufs=1))
+        psum = ctx.enter_context(tc.psum_pool(name="psum", bufs=1))
         ctx.enter_context(tc.manual_schedule())
 
         def ring(name, depth, index, shape, dtype):
-            return sb.tile(shape, dtype, name=name, tag="%s%d" % (name, index % depth), align_bytes=64)
+            return sbuf.tile(shape, dtype, name=name, tag="%s%d" % (name, index % depth), align_bytes=64)
+
+        def y_buffer(index, shape, dtype):
+            return ring("y", 2 * PAIRS, index, shape, dtype)
+
+        def rounded_buffer(index, shape):
+            return ring("rounded", 6, index, shape, BF16)
+
+        def prob_buffer(index, shape, dtype):
+            return ring("prob", 3, index, shape, dtype)
 
         def bank(index):
-            return ps.tile([P, BANK], F32, name="bank", tag="bank%d" % index)
+            return psum.tile([P, BANK], F32, name="bank", tag="bank%d" % index)
 
         def copy_on(engine, out, in_):
             if engine == "scalar":
@@ -48,345 +59,321 @@ def tile_distill_logit_grad_g1_kernel(tc, h_student, w_student, h_teacher, w_tea
             else:
                 nc.vector.tensor_copy(out=out, in_=in_)
 
-        ident = sb.tile([P, P], F32, name="ident")
+        def quantize(codes, scales, first, packed):
+            cols = slice(first, first + packed.shape[1] // PACK)
+            nc.vector.quantize_mx(out=codes[:, cols].bitcast(FP8X4), scales=scales[:, cols], in_=packed)
+
+        ident = sbuf.tile([P, P], F32, name="ident")
         make_identity(nc, ident[:])
-        warm_in = sb.tile([P, 1], F32, name="warm_in")
-        warm_out = sb.tile([P, 1], F32, name="warm_out")
-        nc.vector.memset(warm_in[:], 0.0)
-        nc.scalar.activation(out=warm_out[:], in_=warm_in[:], func=SIGMOID)
 
-        h_raw, h_banks, h_grouped, h_codes, h_scales = {}, {}, {}, {}, {}
-        w_raw, w_grouped, w_codes, w_scales, cw = {}, {}, {}, {}, {}
-        logits, probs, diffs, ys, y_pairs, y_banks, y_grouped, y_codes, y_scales = {}, {}, {}, {}, {}, {}, {}, {}, {}
-
-        def load_hs(m):
-            t = ring("ybf", 6, m, [P, DS], BF16) if m < 6 else ring("hs", 2, m, [P, DS], BF16)
-            nc.sync.dma_start(out=t[:], in_=h_student[m * P:(m + 1) * P, :])
-            h_raw[m, 0] = t[:].bitcast(F32)
-
-        def load_ht(m):
-            t = ring("ht", 4, m, [P, DT], BF16) if m < 4 else ring("y", 8, m, [P, DT], BF16)
-            nc.sync.dma_start(out=t[:], in_=h_teacher[m * P:(m + 1) * P, :])
-            words = t[:].bitcast(F32)
-            h_raw[m, 1] = words[:, 0:BANK]
-            h_raw[m, 2] = words[:, BANK:2 * BANK]
-
-        def load_w(g, k):
-            source, row = (w_student, k) if k < S_PASSES else (w_teacher, k - S_PASSES)
-            rows = source[row * K_PASS:(row + 1) * K_PASS, g * GROUP:(g + 1) * GROUP]
-            t = ring("wraw", 8, g * PASSES + k, [P, PACK, GROUP], BF16)
-            nc.sync.dma_start(out=t[:], in_=rows.rearrange("(p j) c -> p j c", j=PACK))
-            for i in range(2):
-                w_raw[2 * g + i, k] = t[:, :, i * CHUNK:(i + 1) * CHUNK]
+        factor = sbuf.tile([P, V], BF16, name="factor")
 
         def spread_class_w():
-            spread = sb.tile([P, V], BF16, name="cw")
-            words = class_w.bitcast(F32)
             for part, (first, per) in enumerate(((0, 4), (4 * P, 2))):
-                column = sb.tile([P, per], F32, name="cw_column", tag="cw_column%d" % part)
-                nc.sync.dma_start(out=column[:], in_=words[first:first + per * P].rearrange("(p c) -> p c", c=per))
-                t = bank(6 + part)
+                words = slice(first, first + per * P)
+                column = ring("column", 2, part, [P, per], F32)
+                nc.sync.dma_start(out=column[:], in_=class_w.bitcast(F32)[words].rearrange("(p c) -> p c", c=per))
+                rows = bank(6 + part)
                 for c in range(per):
-                    nc.tensor.transpose(t[:, c * P:(c + 1) * P], column[:, c:c + 1].to_broadcast([P, P]), ident[:])
-                nc.vector.tensor_copy(
-                    out=spread[:].bitcast(F32)[:, first:first + per * P].rearrange("q (p c) -> q p c", c=per),
-                    in_=t[:, 0:per * P].rearrange("q (c p) -> q p c", p=P),
+                    nc.tensor.transpose(rows[:, c * P:(c + 1) * P], column[:, c:c + 1].to_broadcast([P, P]), ident[:])
+                nc.scalar.copy(
+                    out=factor[:].bitcast(F32)[:, words].rearrange("q (p c) -> q p c", c=per),
+                    in_=rows[:, 0:per * P].rearrange("q (c p) -> q p c", p=P),
                 )
-            for g in range(GROUPS):
-                cw[g] = spread[:, g * GROUP:(g + 1) * GROUP]
 
-        def turn_h(m, b):
-            t = bank(len(h_banks) % 3)
-            for g2 in range(2):
-                for u in range(2):
-                    col = (2 * g2 + u) * P
-                    nc.tensor.transpose(t[:, col:col + P], h_raw[m, b][:, 2 * P * g2 + u:2 * P * (g2 + 1):2], ident[:])
-            h_banks[m, b] = t
+        h_words, h_banks, h_packed, h_codes, h_scales = {}, {}, {}, {}, {}
 
-        def group_h(m, b):
-            t = ring("hgr", 4, len(h_grouped), [P, 2 * K_PASS], BF16)
-            nc.scalar.copy(
-                out=t[:].bitcast(F32).rearrange("p (g r u) -> p g r u", g=2, u=2),
-                in_=h_banks[m, b][:].rearrange("p (g u r) -> p g r u", g=2, u=2),
-            )
-            h_grouped[m, b] = t
+        def load_h(m, passes):
+            if passes == STUDENT:
+                source = h_student
+                raw = rounded_buffer(m, [P, DS]) if m < 6 else prob_buffer(m, [P, DS], BF16)
+            else:
+                source = h_teacher
+                raw = ring("teacher", PAIRS, m, [P, DT], BF16) if m < PAIRS else y_buffer(m, [P, DT], BF16)
+            nc.sync.dma_start(out=raw[:], in_=source[m * P:(m + 1) * P, :])
+            h_words[m, passes] = raw[:].bitcast(F32)
 
-        def quantize_h(m, b):
-            if b == 0:
-                h_codes[m] = ring("hq", M_TILES, m, [P, PASSES * P], U32)
-                h_scales[m] = ring("hsc", M_TILES, m, [P, PASSES * P], U8)
-            cols = slice(2 * P * b, 2 * P * (b + 1))
-            nc.vector.quantize_mx(out=h_codes[m][:, cols].bitcast(FP8X4), scales=h_scales[m][:, cols], in_=h_grouped[m, b][:])
+        def turn_h(m, passes):
+            for first in range(0, len(passes), 2):
+                t = bank(len(h_banks) % 3)
+                h_banks[m, passes[first]] = t
+                for g in range(2):
+                    for u in range(2):
+                        col, word = (2 * g + u) * P, 2 * P * (first + g)
+                        nc.tensor.transpose(t[:, col:col + P], h_words[m, passes][:, word + u:word + 2 * P:2], ident[:])
 
-        def group_w(c, k, engine):
-            t = ring("wgr", 5, len(w_grouped), [P, CHUNK * PACK], BF16)
+        def pack_h(m, passes):
+            h_packed[m, passes] = ring("h_packed", 3, len(h_packed), [P, len(passes) * K_PASS], BF16)
+            words = h_packed[m, passes][:].bitcast(F32)
+            for first in range(0, len(passes), 2):
+                nc.scalar.copy(
+                    out=words[:, first * 2 * P:first * 2 * P + BANK].rearrange("p (g s u) -> p g s u", g=2, u=2),
+                    in_=h_banks[m, passes[first]][:].rearrange("p (g u s) -> p g s u", g=2, u=2),
+                )
+
+        def quantize_h(m, passes):
+            if passes == STUDENT:
+                h_codes[m] = ring("h_codes", TILES, m, [P, PASSES * P], U32)
+                h_scales[m] = ring("h_scales", TILES, m, [P, PASSES * P], U8)
+            quantize(h_codes[m], h_scales[m], passes[0] * P, h_packed[m, passes][:])
+
+        w_raw, w_packed = {}, {}
+        w_codes = [ring("w_codes", GROUPS, g, [P, PASSES * GROUP], U32) for g in range(GROUPS)]
+        w_scales = [ring("w_scales", GROUPS, g, [P, PASSES * GROUP], U8) for g in range(GROUPS)]
+
+        def load_w(g, k):
+            source, row = (w_student, k) if k in STUDENT else (w_teacher, k - len(STUDENT))
+            rows = source[row * K_PASS:(row + 1) * K_PASS, g * GROUP:(g + 1) * GROUP]
+            w_raw[g, k] = ring("w_raw", PASSES, k, [P, PACK, GROUP], BF16)
+            nc.sync.dma_start(out=w_raw[g, k][:], in_=rows.rearrange("(p t) c -> p t c", t=PACK))
+
+        def pack_w(g, k, col, width, engine):
+            key = (g, k, col if g == LAST else 0)
+            if key not in w_packed:
+                w_packed[key] = ring("w_packed", 4, len(w_packed), [P, (width if g == LAST else GROUP) * PACK], BF16)
             copy_on(
                 engine,
-                t[:].rearrange("p (c i t) -> p c t i", i=4, t=PACK),
-                w_raw[c, k].rearrange("p t (c i) -> p c t i", i=4),
+                w_packed[key][:, (col - key[2]) * PACK:(col - key[2] + width) * PACK].rearrange("p (c i t) -> p c t i", i=4, t=PACK),
+                w_raw[g, k][:, :, col:col + width].rearrange("p t (c i) -> p c t i", i=4),
             )
-            w_grouped[c, k] = t
 
-        def quantize_w(c, k):
-            if c not in w_codes:
-                w_codes[c] = ring("wq", CHUNKS, c, [P, PASSES * CHUNK], U32)
-                w_scales[c] = ring("wsc", CHUNKS, c, [P, PASSES * CHUNK], U8)
-            cols = slice(k * CHUNK, (k + 1) * CHUNK)
-            nc.vector.quantize_mx(out=w_codes[c][:, cols].bitcast(FP8X4), scales=w_scales[c][:, cols], in_=w_grouped[c, k][:])
+        def quantize_w(g, k, col):
+            quantize(w_codes[g], w_scales[g], k * GROUP + col, w_packed[g, k, col][:])
 
-        def mx_group(out, c, m, passes):
+        logits, probs, diffs, ys = {}, {}, {}, {}
+        first_products = []
+
+        def accumulate(out, m, g, col, passes):
             for k in passes:
-                mc = slice(k * P, (k + 1) * P)
-                vc = slice(k * CHUNK, (k + 1) * CHUNK)
+                samples = slice(k * P, (k + 1) * P)
+                classes = slice(k * GROUP + col, k * GROUP + col + CHUNK)
                 nc.tensor.matmul_mx(
                     out=out,
-                    lhsT=h_codes[m][:, mc].bitcast(FP8X4),
-                    lhsT_scale=h_scales[m][:, mc],
-                    rhs=w_codes[c][:, vc].bitcast(FP8X4),
-                    rhs_scale=w_scales[c][:, vc],
+                    lhsT=h_codes[m][:, samples].bitcast(FP8X4),
+                    lhsT_scale=h_scales[m][:, samples],
+                    rhs=w_codes[g][:, classes].bitcast(FP8X4),
+                    rhs_scale=w_scales[g][:, classes],
                     start=k == passes[0],
                     stop=k == passes[-1],
                 )
 
-        student, teacher = range(S_PASSES), range(S_PASSES, PASSES)
+        def multiply_first_group(m, passes):
+            logits[m] = bank(3 + len(first_products) % 3)
+            first_products.append(m)
+            accumulate(logits[m][:, 0:CHUNK], m, 0, 0, passes)
+            accumulate(logits[m][:, CHUNK:GROUP], m, 0, CHUNK, passes)
 
-        def multiply_first(m, passes):
-            t = bank(3 + m % 3 if passes == student else 3 + (M_TILES + m) % 3)
-            mx_group(t[:, 0:CHUNK], 0, m, passes)
-            mx_group(t[:, CHUNK:2 * CHUNK], 1, m, passes)
-            logits[0, m] = t
+        def multiply_chunk(m, g, col):
+            logits[m] = bank(((g * GROUP + col) // CHUNK * TILES + m) % 6)
+            accumulate(logits[m][:, 0:CHUNK], m, g, col, STUDENT)
+            accumulate(logits[m][:, CHUNK:BANK], m, g, col, TEACHER)
 
-        def multiply(c, m):
-            t = bank((c * M_TILES + m) % 6)
-            mx_group(t[:, 0:CHUNK], c, m, student)
-            mx_group(t[:, CHUNK:2 * CHUNK], c, m, teacher)
-            logits[c, m] = t
+        pairs = [(2 * q, 2 * q + 1) for q in range(PAIRS)]
+        batches = [(0, (m,), 0, GROUP) for m in range(TILES)]
+        batches = batches + [(g, ms, col, CHUNK) for g in range(1, GROUPS) for col in (0, CHUNK) for ms in pairs]
+        batches = batches[:-1] + [(LAST, (m,), CHUNK, CHUNK) for m in pairs[-1]]
 
-        batches = [(0, (m,), 0, GROUP) for m in range(M_TILES)]
-        for c in range(2, CHUNKS):
-            for q in range(M_TILES // 2):
-                if c == CHUNKS - 1 and q == M_TILES // 2 - 1:
-                    batches.append((c // 2, (2 * q,), CHUNK, CHUNK))
-                    batches.append((c // 2, (2 * q + 1,), CHUNK, CHUNK))
-                else:
-                    batches.append((c // 2, (2 * q, 2 * q + 1), (c % 2) * CHUNK, CHUNK))
-
-        def y_part(n):
-            g, ms, col, width = batches[n]
-            j0 = ms[0] % 2
-            return ys[g, ms[0] // 2][:, j0:j0 + len(ms), col:col + width]
-
-        def new_y(g, q):
-            ys[g, q] = ring("y", 8, g * 4 + q, [P, 2, GROUP], F32)
+        def y_part(g, ms, col, width):
+            return ys[g, ms[0] // 2][:, ms[0] % 2:ms[-1] % 2 + 1, col:col + width]
 
         def sigmoid_student(m):
             if m % 2 == 0:
-                new_y(0, m // 2)
-            nc.scalar.activation(out=ys[0, m // 2][:, m % 2, :], in_=logits[0, m][:], func=SIGMOID)
+                ys[0, m // 2] = y_buffer(m // 2, [P, 2, GROUP], F32)
+            nc.scalar.activation(out=ys[0, m // 2][:, m % 2, :], in_=logits[m][:], func=SIGMOID)
 
-        def sigmoid(n, j):
-            g, ms, col, width = batches[n]
-            if j == 0:
-                probs[n] = ring("prob", 3, n, [P, len(ms), BANK], F32)
-            c = 0 if g == 0 else 2 * g + col // CHUNK
-            nc.scalar.activation(out=probs[n][:, j, :], in_=logits[c, ms[j]][:], func=SIGMOID)
+        def sigmoid(b, m):
+            ms = batches[b][1]
+            if m == ms[0]:
+                probs[b] = prob_buffer(b, [P, len(ms), BANK], F32)
+            nc.scalar.activation(out=probs[b][:, m - ms[0], :], in_=logits[m][:], func=SIGMOID)
 
-        def subtract(n):
-            g, ms, col, width = batches[n]
-            diffs[n] = ring("diff", 2, n, [P, len(ms), width], F32)
+        def subtract(b):
+            g, ms, col, width = batches[b]
+            diffs[b] = ring("diff", 2, b, [P, len(ms), width], F32)
             if g == 0:
-                nc.vector.tensor_sub(out=diffs[n][:], in0=y_part(n), in1=probs[n][:])
+                nc.vector.tensor_sub(out=diffs[b][:], in0=y_part(*batches[b]), in1=probs[b][:])
             else:
-                nc.vector.tensor_sub(out=diffs[n][:], in0=probs[n][:, :, 0:CHUNK], in1=probs[n][:, :, CHUNK:2 * CHUNK])
+                nc.vector.tensor_sub(out=diffs[b][:], in0=probs[b][:, :, 0:CHUNK], in1=probs[b][:, :, CHUNK:BANK])
 
-        def weigh(n):
-            g, ms, col, width = batches[n]
+        def weigh(b):
+            g, ms, col, width = batches[b]
             if g > 0 and col == 0:
-                new_y(g, ms[0] // 2)
-            factor = cw[g][:, col:col + width].unsqueeze(1).to_broadcast([P, len(ms), width])
-            nc.vector.tensor_mul(out=y_part(n), in0=diffs[n][:], in1=factor)
+                ys[g, ms[0] // 2] = y_buffer(g * PAIRS + ms[0] // 2, [P, 2, GROUP], F32)
+            row = factor[:, g * GROUP + col:g * GROUP + col + width]
+            nc.vector.tensor_mul(
+                out=y_part(*batches[b]), in0=diffs[b][:], in1=row.unsqueeze(1).to_broadcast([P, len(ms), width])
+            )
 
-        def store_y(n):
-            g, ms, col, width = batches[n]
-            q = ms[0] // 2
-            if g == GROUPS - 1:
-                rows = out_0[ms[0] * P:(ms[-1] + 1) * P, g * GROUP + col:g * GROUP + col + width]
-                nc.sync.dma_start(out=rows.rearrange("(j p) v -> p j v", p=P), in_=y_part(n))
-            elif ms[-1] % 2 == 1 and col + width == GROUP:
-                rows = out_0[2 * q * P:(2 * q + 2) * P, g * GROUP:(g + 1) * GROUP]
-                nc.sync.dma_start(out=rows.rearrange("(j p) v -> p j v", p=P), in_=ys[g, q][:])
+        def store_y(g, ms, col, width):
+            rows = out_0[ms[0] * P:(ms[-1] + 1) * P, g * GROUP + col:g * GROUP + col + width]
+            nc.sync.dma_start(out=rows.rearrange("(j s) v -> s j v", s=P), in_=y_part(g, ms, col, width))
 
-        units = [(g, (2 * q, 2 * q + 1)) for g in range(GROUPS) for q in range(M_TILES // 2)]
-        units = units[:-1] + [(GROUPS - 1, (m,)) for m in units[-1][1]]
+        rounded, y_banks, y_packed = {}, {}, {}
+        y_codes = [ring("y_codes", GROUPS, g, [P, M], U32) for g in range(GROUPS)]
+        y_scales = [ring("y_scales", GROUPS, g, [P, M], U8) for g in range(GROUPS)]
 
         def round_y(g, ms, col, width, engine):
-            j0, q = ms[0] % 2, ms[0] // 2
-            if j0 == 0 and col == 0:
-                y_pairs[g, q] = ring("ybf", 6, g * 4 + q, [P, 2, 2, P, 2], BF16)
+            if ms[0] % 2 == 0 and col == 0:
+                rounded[g, ms[0] // 2] = rounded_buffer(g * PAIRS + ms[0] // 2, [P, 2, 2, P, 2])
             copy_on(
                 engine,
-                y_pairs[g, q][:, j0:j0 + len(ms), :, col // PACK:(col + width) // PACK, :],
-                ys[g, q][:, j0:j0 + len(ms), col:col + width].rearrange("m j (p u e) -> m j u p e", u=2, e=2),
+                rounded[g, ms[0] // 2][:, ms[0] % 2:ms[-1] % 2 + 1, :, col // PACK:(col + width) // PACK, :],
+                y_part(g, ms, col, width).rearrange("s j (p u e) -> s j u p e", u=2, e=2),
             )
 
-        def turn_y(u):
-            g, ms = units[u]
-            words = y_pairs[g, ms[0] // 2][:].rearrange("m j u p e -> m (j u p e)").bitcast(F32)
-            y_banks[u] = bank(6 + u % 2 if u < 10 else u - 10)
+        def turn_y(g, ms, bank_index):
+            words = rounded[g, ms[0] // 2][:].rearrange("s j u p e -> s (j u p e)").bitcast(F32)
+            y_banks[g, ms] = bank(bank_index)
             for i in range(2 * len(ms)):
-                src = (2 * (ms[0] % 2) + i) * P
-                nc.tensor.transpose(y_banks[u][:, i * P:(i + 1) * P], words[:, src:src + P], ident[:])
+                first = (2 * (ms[0] % 2) + i) * P
+                nc.tensor.transpose(y_banks[g, ms][:, i * P:(i + 1) * P], words[:, first:first + P], ident[:])
 
-        def group_y(u, engine):
-            g, ms = units[u]
-            t = ring("ygr", 3, u, [P, len(ms) * P * PACK], BF16)
-            copy_on(
-                engine,
-                t[:].bitcast(F32).rearrange("p (j m u) -> p j m u", m=P, u=2),
-                y_banks[u][:, 0:2 * P * len(ms)].rearrange("p (j u m) -> p j m u", m=P, u=2),
+        def pack_y(g, ms):
+            y_packed[g, ms] = ring("y_packed", 3, len(y_packed), [P, len(ms) * P * PACK], BF16)
+            nc.scalar.copy(
+                out=y_packed[g, ms][:].bitcast(F32).rearrange("p (j s u) -> p j s u", s=P, u=2),
+                in_=y_banks[g, ms][:, 0:2 * P * len(ms)].rearrange("p (j u s) -> p j s u", s=P, u=2),
             )
-            y_grouped[u] = t
 
-        def quantize_y(u):
-            g, ms = units[u]
-            if ms[0] == 0:
-                y_codes[g] = ring("yq", GROUPS, g, [P, M], U32)
-                y_scales[g] = ring("ysc", GROUPS, g, [P, M], U8)
-            cols = slice(ms[0] * P, (ms[-1] + 1) * P)
-            nc.vector.quantize_mx(out=y_codes[g][:, cols].bitcast(FP8X4), scales=y_scales[g][:, cols], in_=y_grouped[u][:])
+        last_stores = {3: 0, 5: 4, 7: 6}
 
-        def store_planes(u):
-            g, ms = units[u]
-            last = ms[-1] == M_TILES - 1
-            words = out_1[g].rearrange("p m t -> p (m t)").bitcast(I32)
-            if g == GROUPS - 1:
-                if ms[-1] in {3: 0, 5: 4, 7: 6}:
-                    cols = slice({3: 0, 5: 4, 7: 6}[ms[-1]] * P, (ms[-1] + 1) * P)
-                    nc.sync.dma_start(out=words[:, cols], in_=y_codes[g][:, cols].bitcast(I32))
-            elif last:
-                nc.sync.dma_start(out=words, in_=y_codes[g][:].bitcast(I32))
-            if last:
+        def quantize_y(g, ms):
+            quantize(y_codes[g], y_scales[g], ms[0] * P, y_packed[g, ms][:])
+            complete = ms[-1] == TILES - 1
+            if complete or (g == LAST and ms[-1] in last_stores):
+                cols = slice(last_stores[ms[-1]] * P if g == LAST else 0, (ms[-1] + 1) * P)
+                words = out_1[g].rearrange("p s t -> p (s t)").bitcast(I32)
+                nc.sync.dma_start(out=words[:, cols], in_=y_codes[g][:, cols].bitcast(I32))
+            if complete:
                 for quad in range(4):
-                    queue = nc.scalar if g == GROUPS - 1 and quad % 2 == 0 else nc.sync
+                    queue = nc.scalar if g == LAST and quad % 2 == 0 else nc.sync
                     queue.dma_start(
                         out=out_2[g, 4 * quad:4 * quad + 4, :].bitcast(I32),
                         in_=y_scales[g][32 * quad:32 * quad + 4, :].bitcast(I32),
                     )
 
         spread_class_w()
-        load_hs(0)
         load_w(0, 0)
+        load_h(0, STUDENT)
         load_w(0, 1)
-        load_hs(1)
-        turn_h(0, 0)
-        group_h(0, 0)
-        for s in range(1, M_TILES // 2):
-            load_hs(2 * s)
-            load_hs(2 * s + 1)
-            load_w(0, S_PASSES + s - 1)
-        load_ht(0)
-        load_w(0, PASSES - 1)
-        load_ht(1)
+        load_h(1, STUDENT)
+        for q in range(1, PAIRS):
+            load_h(2 * q, STUDENT)
+            load_h(2 * q + 1, STUDENT)
+            load_w(0, TEACHER[q - 1])
+        load_h(0, TEACHER)
+        load_w(0, TEACHER[-1])
+        load_h(1, TEACHER)
+
+        turn_h(0, STUDENT)
+        pack_h(0, STUDENT)
+        pack_w(0, 0, 0, GROUP, "vector")
+        pack_w(0, 1, CHUNK, CHUNK, "scalar")
+        quantize_w(0, 0, 0)
+        pack_w(0, 1, 0, CHUNK, "vector")
+        quantize_h(0, STUDENT)
+        turn_h(1, STUDENT)
+        pack_h(1, STUDENT)
         load_w(1, 0)
-
-        group_w(0, 0, "vector")
-        group_w(1, 0, "scalar")
-        quantize_h(0, 0)
-        quantize_w(0, 0)
-        group_w(0, 1, "vector")
-        quantize_w(1, 0)
-        group_w(1, 1, "scalar")
-        turn_h(1, 0)
-        group_h(1, 0)
-        quantize_w(0, 1)
-        quantize_w(1, 1)
-        quantize_h(1, 0)
-        for m in range(M_TILES):
-            ahead = [(m + 2, 0)] if m + 2 < M_TILES else [(m + 2 - M_TILES, 1), (m + 2 - M_TILES, 2)]
-            for mm, b in ahead:
-                turn_h(mm, b)
-                group_h(mm, b)
-            multiply_first(m, student)
+        quantize_w(0, 1, 0)
+        quantize_h(1, STUDENT)
+        for m in range(TILES):
+            ahead = (m + 2, STUDENT) if m + 2 < TILES else (m + 2 - TILES, TEACHER)
+            turn_h(*ahead)
+            multiply_first_group(m, STUDENT)
+            if m > 0:
+                pack_h(*ahead)
             sigmoid_student(m)
-            c, k = m % 2, S_PASSES + m // 2
-            group_w(c, k, "vector")
-            quantize_h(*ahead[0])
-            quantize_w(c, k)
-            for mm, b in ahead[1:]:
-                quantize_h(mm, b)
+            if m == 0:
+                pack_h(*ahead)
+            if m % 2 == 0:
+                pack_w(0, TEACHER[m // 2], 0, GROUP, "vector")
+            else:
+                quantize_w(0, TEACHER[m // 2], 0)
+            if m == TILES - 1:
+                pack_w(1, 0, 0, GROUP, "vector")
+            quantize_h(*ahead)
 
-
+        first_chunk_step = TILES
         steps = range(len(batches) + 5)
-        pieces = {n: [] for n in steps}
-        for n, c, k, engine in [(0, 2, 0, "scalar"), (0, 3, 0, "vector"), (1, 2, 1, "scalar"), (1, 3, 1, "vector"), (2, 2, 2, "scalar"), (2, 3, 2, "vector"), (3, 2, 3, "scalar"), (3, 3, 3, "vector"), (4, 2, 4, "scalar"), (4, 3, 4, "vector"), (5, 2, 5, "scalar"), (5, 3, 5, "vector"), (6, 4, 0, "scalar"), (7, 4, 1, "scalar"), (8, 4, 2, "vector"), (9, 4, 3, "scalar"), (10, 4, 4, "scalar"), (11, 4, 5, "vector"), (12, 5, 0, "scalar"), (13, 5, 1, "scalar"), (14, 5, 2, "vector"), (15, 5, 3, "scalar"), (16, 5, 4, "scalar"), (17, 5, 5, "vector")]:
-            pieces[n].append((c, k, engine))
-        loads = {0: [(1, 1)], 1: [(1, 2)], 2: [(1, 3)], 3: [(1, 4)], 4: [(1, 5)], 5: [(2, 0), (2, 1), (2, 2), (2, 3), (2, 4), (2, 5)]}
-        rounds = {n: [] for n in steps}
-        turns = {n: [] for n in steps}
-        groups = {n: [] for n in steps}
-        for u, (g, ms) in enumerate(units):
-            if g < GROUPS - 1:
-                n = [8, 9, 11, 12, 14, 15, 17, 18][u]
-                rounds[n].append((g, ms, 0, GROUP, (["vector"] * 8)[u]))
-                turns[[11, 11, 14, 14, 17, 17, 20, 20][u]].append(u)
-                groups[[12, 13, 15, 16, 18, 19, 21, 22][u]].append((u, "scalar"))
-        for n, batch in enumerate(batches):
-            if batch[0] == GROUPS - 1:
-                rounds[n + 2].append(batch + ("scalar" if n in (20, 21, 22) else "vector",))
-                if batch[2] > 0:
-                    u = units.index(batch[:2])
-                    turns[n + 4].append(u)
-                    groups[n + 4 + 1].append((u, "vector" if n in () else "scalar"))
+        subtractions, products, packs, rounds, turns, plane_packs = ({n: [] for n in steps} for kind in range(6))
+        for b, (g, ms, col, width) in enumerate(batches):
+            done = b
+            subtractions[done + 1].append(b)
+            products[done + 1].append(b)
+            if g == LAST:
+                rounds[done + 2].append((g, ms, col, width, "scalar" if col > 0 and len(ms) == 2 else "vector"))
+                if col > 0:
+                    late = ms[0] // 2 >= 2
+                    turns[done + 4].append((g, ms, ms[-1] - 5 if late else 6 + ms[0] // 2))
+                    plane_packs[done + 5].append((g, ms))
+        for i, (g, ms) in enumerate([(g, ms) for g in range(LAST) for ms in pairs]):
+            n = first_chunk_step + 3 * (i // 2)
+            rounds[n + i % 2].append((g, ms, 0, GROUP, "vector"))
+            turns[n + 3].append((g, ms, 6 + i % 2))
+            plane_packs[n + 4 + i % 2].append((g, ms))
+        for k in range(1, PASSES):
+            packs[k - 1].append((1, k, CHUNK, "vector", False))
+            packs[k - 1].append((1, k, 0, "scalar", True))
+        for i in range(2 * PASSES):
+            packs[PASSES - 1 + i].append((LAST, i % PASSES, i // PASSES * CHUNK, "vector" if i % 3 == 0 else "scalar", True))
 
-        pending = []
+        waiting = [(1, 0, 0)]
         for n in steps:
-            live = n < len(batches)
-            group = [1, 2] if n + 2 < M_TILES else []
-            if group:
-                load_ht(n + 2)
-            for b in group:
-                turn_h(n + 2, b)
-                group_h(n + 2, b)
-            if n < M_TILES:
-                multiply_first(n, teacher)
-            elif live:
-                g, ms, col, width = batches[n]
-                for m in ms:
-                    multiply(2 * g + col // CHUNK, m)
-            for u in turns[n]:
-                turn_y(u)
-            if live:
-                sigmoid(n, 0)
-            for u, engine in groups[n]:
-                group_y(u, engine)
-            if live and len(batches[n][1]) == 2:
-                sigmoid(n, 1)
-            on_vector = [piece for piece in pieces[n] if piece[2] == "vector"]
-            fill = [lambda cc=cc, k=k: group_w(cc, k, "vector") for cc, k, engine in on_vector]
-            fill.extend([lambda task=task: round_y(*task) for task in rounds[n] if task[-1] == "vector"])
-            fill.extend([lambda cc=cc, k=k: quantize_w(cc, k) for cc, k in pending])
-            fill.extend([lambda u=u: (quantize_y(u), store_planes(u)) for u, engine in groups[n]])
-            fill.extend([lambda b=b: quantize_h(n + 2, b) for b in group])
-            fill.extend([lambda cc=cc, k=k: quantize_w(cc, k) for cc, k, engine in on_vector])
-            pending = []
-            if 0 <= n - 1 < len(batches):
-                subtract(n - 1)
-            for task in fill[:1]:
-                task()
-            if 0 <= n - 1 < len(batches):
-                weigh(n - 1)
-                if n - 1 >= M_TILES:
-                    store_y(n - 1)
-                if 8 <= n < 8 + 4:
-                    store_y(2 * (n - 8) + 1)
-            for task in fill[1:]:
-                task()
+            b = n
+            tiles = batches[b][1] if b < len(batches) else ()
+            if n + 2 < TILES:
+                load_h(n + 2, TEACHER)
+                turn_h(n + 2, TEACHER)
+                pack_h(n + 2, TEACHER)
+            if n + 1 < PASSES:
+                load_w(1, n + 1)
+            if n + 1 == PASSES:
+                for k in range(PASSES):
+                    load_w(LAST, k)
+            for m in tiles:
+                if n < first_chunk_step:
+                    multiply_first_group(m, TEACHER)
+                else:
+                    multiply_chunk(m, batches[b][0], batches[b][2])
+            for task in turns[n]:
+                turn_y(*task)
+            for m in tiles[:1]:
+                sigmoid(b, m)
+            for task in plane_packs[n]:
+                pack_y(*task)
+            for m in tiles[1:]:
+                sigmoid(b, m)
+
+            on_vector = [task for task in packs[n] if task[3] == "vector"]
+            fill = [(pack_w, (g, k, col, CHUNK, "vector")) for g, k, col, engine, whole in on_vector]
+            fill.extend([(round_y, task) for task in rounds[n] if task[-1] == "vector"])
+            fill.extend([(quantize_w, task) for task in waiting])
+            fill.extend([(quantize_y, task) for task in plane_packs[n]])
+            if n + 2 < TILES:
+                fill.append((quantize_h, (n + 2, TEACHER)))
+            fill.extend([(quantize_w, (g, k, col)) for g, k, col, engine, whole in on_vector if whole])
+            for i in subtractions[n]:
+                subtract(i)
+            for call, task in fill[:1]:
+                call(*task)
+            for i in products[n]:
+                weigh(i)
+                g, ms, col, width = batches[i]
+                if g == LAST:
+                    store_y(g, ms, col, width)
+                elif g > 0 and col > 0:
+                    store_y(g, ms, 0, GROUP)
+            if 0 <= n - first_chunk_step < PAIRS:
+                store_y(0, pairs[n - first_chunk_step], 0, GROUP)
+            for call, task in fill[1:]:
+                call(*task)
+
             for task in rounds[n]:
                 if task[-1] == "scalar":
                     round_y(*task)
-            for cc, k, engine in pieces[n]:
+            waiting = []
+            for g, k, col, engine, whole in packs[n]:
                 if engine == "scalar":
-                    group_w(cc, k, engine)
-                    pending.append((cc, k))
-            for g, k in loads.get(n, []):
-                load_w(g, k)
+                    pack_w(g, k, col, CHUNK, engine)
+                    waiting.append((g, k, col))

@@ -68,18 +68,28 @@ def tile_distill_logit_grad_g1_kernel(
 
         factor = sbuf.tile([P, V], BF16, name="factor")
 
+        parts = ((0, 4), (4 * P, 2))
+        columns, rows_of = {}, {}
+
+        def load_class_w():
+            for part, (first, per) in enumerate(parts):
+                columns[part] = ring("column", 2, part, [P, per], F32)
+                words = class_w.bitcast(F32)[first:first + per * P]
+                nc.sync.dma_start(out=columns[part][:], in_=words.rearrange("(p c) -> p c", c=per))
+
         def spread_class_w():
-            for part, (first, per) in enumerate(((0, 4), (4 * P, 2))):
-                words = slice(first, first + per * P)
-                column = ring("column", 2, part, [P, per], F32)
-                nc.sync.dma_start(out=column[:], in_=class_w.bitcast(F32)[words].rearrange("(p c) -> p c", c=per))
-                rows = bank(6 + part)
+            for part, (first, per) in enumerate(parts):
+                rows_of[part] = bank(6 + part)
                 for c in range(per):
-                    nc.tensor.transpose(rows[:, c * P:(c + 1) * P], column[:, c:c + 1].to_broadcast([P, P]), ident[:])
-                nc.scalar.copy(
-                    out=factor[:].bitcast(F32)[:, words].rearrange("q (p c) -> q p c", c=per),
-                    in_=rows[:, 0:per * P].rearrange("q (c p) -> q p c", p=P),
-                )
+                    repeated = columns[part][:, c:c + 1].to_broadcast([P, P])
+                    nc.tensor.transpose(rows_of[part][:, c * P:(c + 1) * P], repeated, ident[:])
+
+        def copy_class_w(part):
+            first, per = parts[part]
+            nc.scalar.copy(
+                out=factor[:].bitcast(F32)[:, first:first + per * P].rearrange("q (p c) -> q p c", c=per),
+                in_=rows_of[part][:, 0:per * P].rearrange("q (c p) -> q p c", p=P),
+            )
 
         h_words, h_banks, h_packed, h_codes, h_scales = {}, {}, {}, {}, {}
 
@@ -133,8 +143,8 @@ def tile_distill_logit_grad_g1_kernel(
                 w_packed[key] = ring("w_packed", 4, len(w_packed), [P, (width if g == LAST else GROUP) * PACK], BF16)
             copy_on(
                 engine,
-                w_packed[key][:, (col - key[2]) * PACK:(col - key[2] + width) * PACK].rearrange("p (c i t) -> p c t i", i=4, t=PACK),
-                w_raw[g, k][:, :, col:col + width].rearrange("p t (c i) -> p c t i", i=4),
+                w_packed[key][:, (col - key[2]) * PACK:(col - key[2] + width) * PACK].rearrange("p (c i t) -> p c t i", i=8, t=PACK),
+                w_raw[g, k][:, :, col:col + width].rearrange("p t (c i) -> p c t i", i=8),
             )
 
         def quantize_w(g, k, col):
@@ -143,10 +153,10 @@ def tile_distill_logit_grad_g1_kernel(
         logits, probs, diffs, ys = {}, {}, {}, {}
         first_products = []
 
-        def accumulate(out, m, g, col, passes):
+        def accumulate(out, m, g, col, width, passes):
             for k in passes:
                 samples = slice(k * P, (k + 1) * P)
-                classes = slice(k * GROUP + col, k * GROUP + col + CHUNK)
+                classes = slice(k * GROUP + col, k * GROUP + col + width)
                 nc.tensor.matmul_mx(
                     out=out,
                     lhsT=h_codes[m][:, samples].bitcast(FP8X4),
@@ -160,13 +170,12 @@ def tile_distill_logit_grad_g1_kernel(
         def multiply_first_group(m, passes):
             logits[m] = bank(3 + len(first_products) % 3)
             first_products.append(m)
-            accumulate(logits[m][:, 0:CHUNK], m, 0, 0, passes)
-            accumulate(logits[m][:, CHUNK:GROUP], m, 0, CHUNK, passes)
+            accumulate(logits[m][:], m, 0, 0, GROUP, passes)
 
         def multiply_chunk(m, g, col):
             logits[m] = bank(((g * GROUP + col) // CHUNK * TILES + m) % 6)
-            accumulate(logits[m][:, 0:CHUNK], m, g, col, STUDENT)
-            accumulate(logits[m][:, CHUNK:BANK], m, g, col, TEACHER)
+            accumulate(logits[m][:, 0:CHUNK], m, g, col, CHUNK, STUDENT)
+            accumulate(logits[m][:, CHUNK:BANK], m, g, col, CHUNK, TEACHER)
 
         pairs = [(2 * q, 2 * q + 1) for q in range(PAIRS)]
         batches = [(0, (m,), 0, GROUP) for m in range(TILES)]
@@ -252,9 +261,9 @@ def tile_distill_logit_grad_g1_kernel(
                         in_=y_scales[g][32 * quad:32 * quad + 4, :].bitcast(I32),
                     )
 
-        spread_class_w()
         load_w(0, 0)
         load_h(0, STUDENT)
+        load_class_w()
         load_w(0, 1)
         load_h(1, STUDENT)
         for q in range(1, PAIRS):
@@ -267,6 +276,7 @@ def tile_distill_logit_grad_g1_kernel(
 
         turn_h(0, STUDENT)
         pack_h(0, STUDENT)
+        spread_class_w()
         pack_w(0, 0, 0, GROUP, "vector")
         pack_w(0, 1, CHUNK, CHUNK, "scalar")
         quantize_w(0, 0, 0)
@@ -293,6 +303,9 @@ def tile_distill_logit_grad_g1_kernel(
             if m == TILES - 1:
                 pack_w(1, 0, 0, GROUP, "vector")
             quantize_h(*ahead)
+
+        for part in range(len(parts)):
+            copy_class_w(part)
 
         first_chunk_step = TILES
         steps = range(len(batches) + 5)

from contextlib import ExitStack

import concourse.mybir as mybir
from concourse.masks import make_identity

M, DS, DT, V = 1024, 1024, 2048, 1536
FLOPS = 2 * M * V * (DS + DT)

F32 = mybir.dt.float32
BF16 = mybir.dt.bfloat16
I32 = mybir.dt.int32
U32 = mybir.dt.uint32
U8 = mybir.dt.uint8
FP8X4 = mybir.dt.float8_e4m3fn_x4
SIGMOID = mybir.ActivationFunctionType.Sigmoid

P = 128
PACK = 4
K_PASS = P * PACK
STUDENT = range(DS // K_PASS)
TEACHER = range(DS // K_PASS, (DS + DT) // K_PASS)
PASSES = len(STUDENT) + len(TEACHER)
TILES = M // P
PAIRS = TILES // 2
GROUP = K_PASS
GROUPS = V // GROUP
LAST = GROUPS - 1
CHUNK = GROUP // 2
BANK = 512


def tile_distill_logit_grad_g1_kernel(
    tc, h_student, w_student, h_teacher, w_teacher, class_w, out_0, out_1, out_2
):
    nc = tc.nc
    with ExitStack() as ctx:
        sbuf = ctx.enter_context(tc.tile_pool(name="sbuf", bufs=1))
        psum = ctx.enter_context(tc.psum_pool(name="psum", bufs=1))
        ctx.enter_context(tc.manual_schedule())

        def ring(name, depth, index, shape, dtype):
            return sbuf.tile(shape, dtype, name=name, tag="%s%d" % (name, index % depth), align_bytes=64)

        def y_buffer(index, shape, dtype):
            return ring("y", 2 * PAIRS, index, shape, dtype)

        def rounded_buffer(index, shape):
            return ring("rounded", 6, index, shape, BF16)

        def prob_buffer(index, shape, dtype):
            return ring("prob", 3, index, shape, dtype)

        def bank(index):
            return psum.tile([P, BANK], F32, name="bank", tag="bank%d" % index)

        def copy_on(engine, out, in_):
            if engine == "scalar":
                nc.scalar.copy(out=out, in_=in_)
            else:
                nc.vector.tensor_copy(out=out, in_=in_)

        def quantize(codes, scales, first, packed):
            cols = slice(first, first + packed.shape[1] // PACK)
            nc.vector.quantize_mx(out=codes[:, cols].bitcast(FP8X4), scales=scales[:, cols], in_=packed)

        ident = sbuf.tile([P, P], F32, name="ident")
        make_identity(nc, ident[:])

        factor = sbuf.tile([P, V], BF16, name="factor")

        parts = ((0, 4), (4 * P, 2))
        columns, rows_of = {}, {}

        def load_class_w():
            for part, (first, per) in enumerate(parts):
                columns[part] = ring("column", 2, part, [P, per], F32)
                words = class_w.bitcast(F32)[first:first + per * P]
                nc.sync.dma_start(out=columns[part][:], in_=words.rearrange("(p c) -> p c", c=per))

        def spread_class_w():
            for part, (first, per) in enumerate(parts):
                rows_of[part] = bank(6 + part)
                for c in range(per):
                    repeated = columns[part][:, c:c + 1].to_broadcast([P, P])
                    nc.tensor.transpose(rows_of[part][:, c * P:(c + 1) * P], repeated, ident[:])

        def copy_class_w(part):
            first, per = parts[part]
            nc.scalar.copy(
                out=factor[:].bitcast(F32)[:, first:first + per * P].rearrange("q (p c) -> q p c", c=per),
                in_=rows_of[part][:, 0:per * P].rearrange("q (c p) -> q p c", p=P),
            )

        h_words, h_banks, h_packed, h_codes, h_scales = {}, {}, {}, {}, {}

        def load_h(m, passes):
            if passes == STUDENT:
                source = h_student
                raw = rounded_buffer(m, [P, DS]) if m < 6 else prob_buffer(m, [P, DS], BF16)
            else:
                source = h_teacher
                raw = ring("teacher", PAIRS, m, [P, DT], BF16) if m < PAIRS else y_buffer(m, [P, DT], BF16)
            nc.sync.dma_start(out=raw[:], in_=source[m * P:(m + 1) * P, :])
            h_words[m, passes] = raw[:].bitcast(F32)

        def turn_h(m, passes):
            for first in range(0, len(passes), 2):
                t = bank(len(h_banks) % 3)
                h_banks[m, passes[first]] = t
                for g in range(2):
                    for u in range(2):
                        col, word = (2 * g + u) * P, 2 * P * (first + g)
                        nc.tensor.transpose(t[:, col:col + P], h_words[m, passes][:, word + u:word + 2 * P:2], ident[:])

        def pack_h(m, passes):
            h_packed[m, passes] = ring("h_packed", 3, len(h_packed), [P, len(passes) * K_PASS], BF16)
            words = h_packed[m, passes][:].bitcast(F32)
            for first in range(0, len(passes), 2):
                nc.scalar.copy(
                    out=words[:, first * 2 * P:first * 2 * P + BANK].rearrange("p (g s u) -> p g s u", g=2, u=2),
                    in_=h_banks[m, passes[first]][:].rearrange("p (g u s) -> p g s u", g=2, u=2),
                )

        def quantize_h(m, passes):
            if passes == STUDENT:
                h_codes[m] = ring("h_codes", TILES, m, [P, PASSES * P], U32)
                h_scales[m] = ring("h_scales", TILES, m, [P, PASSES * P], U8)
            quantize(h_codes[m], h_scales[m], passes[0] * P, h_packed[m, passes][:])

        w_raw, w_packed = {}, {}
        w_codes = [ring("w_codes", GROUPS, g, [P, PASSES * GROUP], U32) for g in range(GROUPS)]
        w_scales = [ring("w_scales", GROUPS, g, [P, PASSES * GROUP], U8) for g in range(GROUPS)]

        def load_w(g, k):
            source, row = (w_student, k) if k in STUDENT else (w_teacher, k - len(STUDENT))
            rows = source[row * K_PASS:(row + 1) * K_PASS, g * GROUP:(g + 1) * GROUP]
            w_raw[g, k] = ring("w_raw", PASSES, k, [P, PACK, GROUP], BF16)
            nc.sync.dma_start(out=w_raw[g, k][:], in_=rows.rearrange("(p t) c -> p t c", t=PACK))

        def pack_w(g, k, col, width, engine):
            key = (g, k, col if g == LAST else 0)
            if key not in w_packed:
                w_packed[key] = ring("w_packed", 4, len(w_packed), [P, (width if g == LAST else GROUP) * PACK], BF16)
            copy_on(
                engine,
                w_packed[key][:, (col - key[2]) * PACK:(col - key[2] + width) * PACK].rearrange("p (c i t) -> p c t i", i=8, t=PACK),
                w_raw[g, k][:, :, col:col + width].rearrange("p t (c i) -> p c t i", i=8),
            )

        def quantize_w(g, k, col):
            quantize(w_codes[g], w_scales[g], k * GROUP + col, w_packed[g, k, col][:])

        logits, probs, diffs, ys = {}, {}, {}, {}
        first_products = []

        def accumulate(out, m, g, col, width, passes):
            for k in passes:
                samples = slice(k * P, (k + 1) * P)
                classes = slice(k * GROUP + col, k * GROUP + col + width)
                nc.tensor.matmul_mx(
                    out=out,
                    lhsT=h_codes[m][:, samples].bitcast(FP8X4),
                    lhsT_scale=h_scales[m][:, samples],
                    rhs=w_codes[g][:, classes].bitcast(FP8X4),
                    rhs_scale=w_scales[g][:, classes],
                    start=k == passes[0],
                    stop=k == passes[-1],
                )

        def multiply_first_group(m, passes):
            logits[m] = bank(3 + len(first_products) % 3)
            first_products.append(m)
            accumulate(logits[m][:], m, 0, 0, GROUP, passes)

        def multiply_chunk(m, g, col):
            logits[m] = bank(((g * GROUP + col) // CHUNK * TILES + m) % 6)
            accumulate(logits[m][:, 0:CHUNK], m, g, col, CHUNK, STUDENT)
            accumulate(logits[m][:, CHUNK:BANK], m, g, col, CHUNK, TEACHER)

        pairs = [(2 * q, 2 * q + 1) for q in range(PAIRS)]
        batches = [(0, (m,), 0, GROUP) for m in range(TILES)]
        batches = batches + [(g, ms, col, CHUNK) for g in range(1, GROUPS) for col in (0, CHUNK) for ms in pairs]
        batches = batches[:-1] + [(LAST, (m,), CHUNK, CHUNK) for m in pairs[-1]]

        def y_part(g, ms, col, width):
            return ys[g, ms[0] // 2][:, ms[0] % 2:ms[-1] % 2 + 1, col:col + width]

        def sigmoid_student(m):
            if m % 2 == 0:
                ys[0, m // 2] = y_buffer(m // 2, [P, 2, GROUP], F32)
            nc.scalar.activation(out=ys[0, m // 2][:, m % 2, :], in_=logits[m][:], func=SIGMOID)

        def sigmoid(b, m):
            ms = batches[b][1]
            if m == ms[0]:
                probs[b] = prob_buffer(b, [P, len(ms), BANK], F32)
            nc.scalar.activation(out=probs[b][:, m - ms[0], :], in_=logits[m][:], func=SIGMOID)

        def subtract(b):
            g, ms, col, width = batches[b]
            diffs[b] = ring("diff", 2, b, [P, len(ms), width], F32)
            if g == 0:
                nc.vector.tensor_sub(out=diffs[b][:], in0=y_part(*batches[b]), in1=probs[b][:])
            else:
                nc.vector.tensor_sub(out=diffs[b][:], in0=probs[b][:, :, 0:CHUNK], in1=probs[b][:, :, CHUNK:BANK])

        def weigh(b):
            g, ms, col, width = batches[b]
            if g > 0 and col == 0:
                ys[g, ms[0] // 2] = y_buffer(g * PAIRS + ms[0] // 2, [P, 2, GROUP], F32)
            row = factor[:, g * GROUP + col:g * GROUP + col + width]
            nc.vector.tensor_mul(
                out=y_part(*batches[b]), in0=diffs[b][:], in1=row.unsqueeze(1).to_broadcast([P, len(ms), width])
            )

        def store_y(g, ms, col, width):
            rows = out_0[ms[0] * P:(ms[-1] + 1) * P, g * GROUP + col:g * GROUP + col + width]
            nc.sync.dma_start(out=rows.rearrange("(j s) v -> s j v", s=P), in_=y_part(g, ms, col, width))

        rounded, y_banks, y_packed = {}, {}, {}
        y_codes = [ring("y_codes", GROUPS, g, [P, M], U32) for g in range(GROUPS)]
        y_scales = [ring("y_scales", GROUPS, g, [P, M], U8) for g in range(GROUPS)]

        def round_y(g, ms, col, width, engine):
            if ms[0] % 2 == 0 and col == 0:
                rounded[g, ms[0] // 2] = rounded_buffer(g * PAIRS + ms[0] // 2, [P, 2, 2, P, 2])
            copy_on(
                engine,
                rounded[g, ms[0] // 2][:, ms[0] % 2:ms[-1] % 2 + 1, :, col // PACK:(col + width) // PACK, :],
                y_part(g, ms, col, width).rearrange("s j (p u e) -> s j u p e", u=2, e=2),
            )

        def turn_y(g, ms, bank_index):
            words = rounded[g, ms[0] // 2][:].rearrange("s j u p e -> s (j u p e)").bitcast(F32)
            y_banks[g, ms] = bank(bank_index)
            for i in range(2 * len(ms)):
                first = (2 * (ms[0] % 2) + i) * P
                nc.tensor.transpose(y_banks[g, ms][:, i * P:(i + 1) * P], words[:, first:first + P], ident[:])

        def pack_y(g, ms):
            y_packed[g, ms] = ring("y_packed", 3, len(y_packed), [P, len(ms) * P * PACK], BF16)
            nc.scalar.copy(
                out=y_packed[g, ms][:].bitcast(F32).rearrange("p (j s u) -> p j s u", s=P, u=2),
                in_=y_banks[g, ms][:, 0:2 * P * len(ms)].rearrange("p (j u s) -> p j s u", s=P, u=2),
            )

        last_stores = {3: 0, 5: 4, 7: 6}

        def quantize_y(g, ms):
            quantize(y_codes[g], y_scales[g], ms[0] * P, y_packed[g, ms][:])
            complete = ms[-1] == TILES - 1
            if complete or (g == LAST and ms[-1] in last_stores):
                cols = slice(last_stores[ms[-1]] * P if g == LAST else 0, (ms[-1] + 1) * P)
                words = out_1[g].rearrange("p s t -> p (s t)").bitcast(I32)
                nc.sync.dma_start(out=words[:, cols], in_=y_codes[g][:, cols].bitcast(I32))
            if complete:
                for quad in range(4):
                    queue = nc.scalar if g == LAST and quad % 2 == 0 else nc.sync
                    queue.dma_start(
                        out=out_2[g, 4 * quad:4 * quad + 4, :].bitcast(I32),
                        in_=y_scales[g][32 * quad:32 * quad + 4, :].bitcast(I32),
                    )

        load_w(0, 0)
        load_h(0, STUDENT)
        load_class_w()
        load_w(0, 1)
        load_h(1, STUDENT)
        for q in range(1, PAIRS):
            load_h(2 * q, STUDENT)
            load_h(2 * q + 1, STUDENT)
            load_w(0, TEACHER[q - 1])
        load_h(0, TEACHER)
        load_w(0, TEACHER[-1])
        load_h(1, TEACHER)

        turn_h(0, STUDENT)
        pack_h(0, STUDENT)
        spread_class_w()
        pack_w(0, 0, 0, GROUP, "vector")
        pack_w(0, 1, CHUNK, CHUNK, "scalar")
        quantize_w(0, 0, 0)
        pack_w(0, 1, 0, CHUNK, "vector")
        quantize_h(0, STUDENT)
        turn_h(1, STUDENT)
        pack_h(1, STUDENT)
        load_w(1, 0)
        quantize_w(0, 1, 0)
        quantize_h(1, STUDENT)
        for m in range(TILES):
            ahead = (m + 2, STUDENT) if m + 2 < TILES else (m + 2 - TILES, TEACHER)
            turn_h(*ahead)
            multiply_first_group(m, STUDENT)
            if m > 0:
                pack_h(*ahead)
            sigmoid_student(m)
            if m == 0:
                pack_h(*ahead)
            if m % 2 == 0:
                pack_w(0, TEACHER[m // 2], 0, GROUP, "vector")
            else:
                quantize_w(0, TEACHER[m // 2], 0)
            if m == TILES - 1:
                pack_w(1, 0, 0, GROUP, "vector")
            quantize_h(*ahead)

        for part in range(len(parts)):
            copy_class_w(part)

        first_chunk_step = TILES
        steps = range(len(batches) + 5)
        subtractions, products, packs, rounds, turns, plane_packs = ({n: [] for n in steps} for kind in range(6))
        for b, (g, ms, col, width) in enumerate(batches):
            done = b
            subtractions[done + 1].append(b)
            products[done + 1].append(b)
            if g == LAST:
                rounds[done + 2].append((g, ms, col, width, "scalar" if col > 0 and len(ms) == 2 else "vector"))
                if col > 0:
                    late = ms[0] // 2 >= 2
                    turns[done + 4].append((g, ms, ms[-1] - 5 if late else 6 + ms[0] // 2))
                    plane_packs[done + 5].append((g, ms))
        for i, (g, ms) in enumerate([(g, ms) for g in range(LAST) for ms in pairs]):
            n = first_chunk_step + 3 * (i // 2)
            rounds[n + i % 2].append((g, ms, 0, GROUP, "vector"))
            turns[n + 3].append((g, ms, 6 + i % 2))
            plane_packs[n + 4 + i % 2].append((g, ms))
        for k in range(1, PASSES):
            packs[k - 1].append((1, k, CHUNK, "vector", False))
            packs[k - 1].append((1, k, 0, "scalar", True))
        for i in range(2 * PASSES):
            packs[PASSES - 1 + i].append((LAST, i % PASSES, i // PASSES * CHUNK, "vector" if i % 3 == 0 else "scalar", True))

        waiting = [(1, 0, 0)]
        for n in steps:
            b = n
            tiles = batches[b][1] if b < len(batches) else ()
            if n + 2 < TILES:
                load_h(n + 2, TEACHER)
                turn_h(n + 2, TEACHER)
                pack_h(n + 2, TEACHER)
            if n + 1 < PASSES:
                load_w(1, n + 1)
            if n + 1 == PASSES:
                for k in range(PASSES):
                    load_w(LAST, k)
            for m in tiles:
                if n < first_chunk_step:
                    multiply_first_group(m, TEACHER)
                else:
                    multiply_chunk(m, batches[b][0], batches[b][2])
            for task in turns[n]:
                turn_y(*task)
            for m in tiles[:1]:
                sigmoid(b, m)
            for task in plane_packs[n]:
                pack_y(*task)
            for m in tiles[1:]:
                sigmoid(b, m)

            on_vector = [task for task in packs[n] if task[3] == "vector"]
            fill = [(pack_w, (g, k, col, CHUNK, "vector")) for g, k, col, engine, whole in on_vector]
            fill.extend([(round_y, task) for task in rounds[n] if task[-1] == "vector"])
            fill.extend([(quantize_w, task) for task in waiting])
            fill.extend([(quantize_y, task) for task in plane_packs[n]])
            if n + 2 < TILES:
                fill.append((quantize_h, (n + 2, TEACHER)))
            fill.extend([(quantize_w, (g, k, col)) for g, k, col, engine, whole in on_vector if whole])
            for i in subtractions[n]:
                subtract(i)
            for call, task in fill[:1]:
                call(*task)
            for i in products[n]:
                weigh(i)
                g, ms, col, width = batches[i]
                if g == LAST:
                    store_y(g, ms, col, width)
                elif g > 0 and col > 0:
                    store_y(g, ms, 0, GROUP)
            if 0 <= n - first_chunk_step < PAIRS:
                store_y(0, pairs[n - first_chunk_step], 0, GROUP)
            for call, task in fill[1:]:
                call(*task)

            for task in rounds[n]:
                if task[-1] == "scalar":
                    round_y(*task)
            waiting = []
            for g, k, col, engine, whole in packs[n]:
                if engine == "scalar":
                    pack_w(g, k, col, CHUNK, engine)
                    waiting.append((g, k, col))
